import numpy as np
import ml_dtypes


def mxq(x, axis, fmt="e4m3"):
    dtype, down = {"e4m3": (ml_dtypes.float8_e4m3fn, 7), "e5m2": (ml_dtypes.float8_e5m2, 14)}[fmt]
    v = np.moveaxis(np.asarray(x, np.float32).astype(ml_dtypes.bfloat16).astype(np.float64), axis, -1)
    blocks = v.reshape(v.shape[:-1] + (-1, 32))
    amax = np.abs(blocks).max(-1, keepdims=True)
    byte = np.maximum(np.where(amax > 0, np.frexp(amax)[1] - 1 + 127, 0) - down, 1)
    scale = np.exp2(byte - 127.0)
    codes = (blocks / scale).astype(np.float32).astype(dtype).astype(np.float64)
    return np.moveaxis((codes * scale).reshape(v.shape), -1, axis)


WIDE = False


def mx_kscale(k):
    if not WIDE:
        return np.ones(k)
    levels = np.array([10, -10, 5, -5, 0])
    if k % 512:
        return np.exp2(np.random.permutation(np.resize(levels, k // 32))).repeat(32)
    a = np.empty((k // 512, 16))
    for p in range(k // 512):
        a[p, :8] = np.random.permutation(np.resize(levels, 8))
        for g in range(8):
            far = levels[np.abs(levels - a[p, g]) >= 10]
            a[p, g + 8] = far[np.random.randint(len(far))]
    return np.exp2(a.ravel()).repeat(32)


def f64(x):
    return np.asarray(x).astype(np.float64)


def striped(idx):
    return np.tile(np.asarray(idx).reshape(-1, 16).T, (8, 1)).astype(np.uint16)


def unstriped(offs):
    return offs[:16].T.reshape(-1).astype(np.int64)


N, T, D, H, M, G, K = 512, 2048, 512, 512, 128, 1024, 1


def setup_inputs():
    n = np.random.standard_normal
    s = mx_kscale(D)[:, None]
    u = mx_kscale(H)[:, None]
    return {
        "xT": (n((D, T)) * s).astype(np.float32),
        "w1": (n((D, H)) / np.sqrt(D) / s * u[:, 0]).astype(np.float32),
        "w2": (n((H, M)) / np.sqrt(H * K) / u).astype(np.float32),
        "offs": striped(np.random.permutation(T)[:N]),
        "offs2": striped(np.random.randint(0, N, G * K)),
    }


def reference(xT, w1, w2, offs, offs2):
    a = mxq(f64(w1), 0, "e4m3").T @ mxq(f64(xT)[:, unstriped(offs)], 0, "e4m3")
    h = np.maximum(a, 0.0)
    e = h[:, unstriped(offs2)].reshape(H, G, K).sum(-1)
    return mxq(f64(w2), 0, "e4m3").T @ mxq(e, 0, "e4m3")

@@ -1,0 +1,180 @@
+import concourse.mybir as mybir
+
+D, T, N, H, M, G = 512, 2048, 512, 512, 128, 1024
+FLOPS = 2 * D * H * N + 2 * H * M * G
+
+F32 = mybir.dt.float32
+BF16 = mybir.dt.bfloat16
+U32 = mybir.dt.uint32
+U16 = mybir.dt.uint16
+U8 = mybir.dt.uint8
+FP8X4 = mybir.dt.float8_e4m3fn_x4
+COPY = mybir.ActivationFunctionType.Copy
+RELU = mybir.ActivationFunctionType.Relu
+
+P = 128
+PACK = 4
+STRIPE = 16
+HALF_N = N // 2
+HALF_H = H // 2
+HALF_M = P // 2
+HALF_G = G // 2
+WINDOW = N + 32
+PARTS = (256, 256, 256, 128, 128)
+STARTS = tuple(sum(PARTS[:k]) for k in range(len(PARTS) + 1))
+
+
+def tile_attend_hop_pick_kernel(tc, xT, w1, w2, offs, offs2, out):
+    nc = tc.nc
+    with (
+        tc.tile_pool(name="held", bufs=1) as held,
+        tc.psum_pool(name="psum", bufs=1) as psum,
+    ):
+        idx = held.tile([P, N // STRIPE], U16)
+        idx2 = held.tile([P, G // STRIPE], U16)
+
+        x_plane = [held.tile([P, T], F32, name=f"x_plane{t}", align_bytes=64) for t in range(PACK)]
+        x_grouped = held.tile([P, N, PACK], BF16, align_bytes=64)
+        x_codes = held.tile([P, N], U32, align_bytes=64)
+        x_scales = held.tile([P, N], U8, align_bytes=64)
+
+        w1_raw = [held.tile([P, PACK, HALF_H], F32, name=f"w1_raw{k}", align_bytes=64) for k in range(2)]
+        w1_grouped = held.tile([P, PACK, P, PACK], BF16, align_bytes=64)
+        w1_codes = held.tile([P, PACK, P], U32, align_bytes=64)
+        w1_scales = held.tile([P, PACK, P], U8, align_bytes=64)
+
+        w2_raw = held.tile([P, PACK, M], F32, align_bytes=64)
+        w2_grouped = held.tile([P, M, PACK], BF16, align_bytes=64)
+        w2_codes = held.tile([P, M], U32, align_bytes=64)
+        w2_scales = held.tile([P, M], U8, align_bytes=64)
+
+        h_plane = [held.tile([P, WINDOW], F32, name=f"h_plane{t}", align_bytes=64) for t in range(PACK)]
+        e_picked = [
+            [held.tile([P, 2, HALF_G], F32, name=f"e_picked{q}{s}", align_bytes=64) for s in range(2)]
+            for q in range(2)
+        ]
+        e_grouped = held.tile([P, G, PACK], BF16, align_bytes=64)
+        e_codes = [held.tile([P, n], U32, name=f"e_codes{k}", align_bytes=64) for k, n in enumerate(PARTS)]
+        e_scales = [held.tile([P, n], U8, name=f"e_scales{k}", align_bytes=64) for k, n in enumerate(PARTS)]
+        result = held.tile([P, G], F32, align_bytes=64)
+
+        x_rows = xT.rearrange("(p t) n -> p t n", t=PACK)
+        w1_rows = w1.rearrange("(p j) c -> p j c", j=PACK)
+        nc.sync.dma_start(idx[:], offs)
+        nc.sync.dma_start(idx2[:], offs2)
+        for t in range(PACK - 1):
+            nc.sync.dma_start(x_plane[t][:], x_rows[:, t, :])
+        nc.sync.dma_start(w1_raw[0][:], w1_rows[:, :, :HALF_H])
+        nc.sync.dma_start(x_plane[PACK - 1][:], x_rows[:, PACK - 1, :])
+        nc.sync.dma_start(w1_raw[1][:], w1_rows[:, :, HALF_H:])
+        nc.sync.dma_start(w2_raw[:], w2.rearrange("(p j) m -> p j m", j=PACK))
+        for t in range(PACK):
+            nc.gpsimd.memset(h_plane[t][:, N:], 0.0)
+
+        def scalar_copy(dst, src):
+            nc.scalar.activation(dst, src, COPY)
+
+        def quantize(codes, scales, grouped):
+            nc.vector.quantize_mx(
+                out=codes.bitcast(FP8X4),
+                scales=scales,
+                in_=grouped.rearrange("p c j -> p (c j)"),
+            )
+
+        def multiply(bank, left_codes, left_scales, right_codes, right_scales):
+            nc.tensor.matmul_mx(
+                out=bank,
+                lhsT=left_codes.bitcast(FP8X4),
+                lhsT_scale=left_scales,
+                rhs=right_codes.bitcast(FP8X4),
+                rhs_scale=right_scales,
+                start=True,
+                stop=True,
+            )
+
+        def group_w1(k, t0, t1):
+            ms = slice(k * HALF_M, (k + 1) * HALF_M)
+            scalar_copy(
+                w1_grouped[:].rearrange("p t m j -> p m t j")[:, ms, t0:t1, :],
+                w1_raw[k][:].rearrange("p j (m t) -> p m t j", t=PACK)[:, :, t0:t1, :],
+            )
+
+        def quantize_w1(t, k):
+            ms = slice(k * HALF_M, (k + 1) * HALF_M)
+            quantize(w1_codes[:, t, ms], w1_scales[:, t, ms], w1_grouped[:, t, ms, :])
+
+        for t in range(PACK - 1):
+            nc.vector.tensor_copy(x_grouped[:, :, t], x_plane[t][:].indirect(idx[:]))
+        group_w1(0, 0, PACK)
+        for t in range(PACK):
+            quantize_w1(t, 0)
+        n_halves = [slice(a * HALF_N, (a + 1) * HALF_N) for a in range(2)]
+        for cols in n_halves:
+            entries = idx[:, cols.start // STRIPE : cols.stop // STRIPE]
+            nc.vector.tensor_copy(x_grouped[:, cols, PACK - 1], x_plane[PACK - 1][:].indirect(entries))
+        group_w1(1, 0, 1)
+        group_w1(1, 1, PACK)
+
+        def quantize_x(cols):
+            quantize(x_codes[:, cols], x_scales[:, cols], x_grouped[:, cols, :])
+
+        def first_product(bank, t, cols):
+            multiply(bank, w1_codes[:, t, :], w1_scales[:, t, :], x_codes[:, cols], x_scales[:, cols])
+
+        quantize_x(n_halves[0])
+        quantize_w1(0, 1)
+        quantize_x(n_halves[1])
+        bank_halves = [psum.tile([P, HALF_N], F32, name=f"bank_half{a}") for a in range(2)]
+        for bank, cols in zip(bank_halves, n_halves):
+            first_product(bank[:], 0, cols)
+        nc.scalar.activation(h_plane[0][:, n_halves[0]], bank_halves[0][:], RELU)
+        for t in range(1, PACK):
+            quantize_w1(t, 1)
+        nc.vector.tensor_relu(h_plane[0][:, n_halves[1]], bank_halves[1][:])
+        for t in range(1, PACK):
+            bank = psum.tile([P, N], F32, name=f"bank{t}")
+            first_product(bank[:], t, slice(0, N))
+            nc.scalar.activation(h_plane[t][:, :N], bank[:], RELU)
+
+        scalar_copy(w2_grouped[:], w2_raw[:].rearrange("p j m -> p m j"))
+        quantize(w2_codes[:], w2_scales[:], w2_grouped[:])
+
+        def pick(t, lo, hi):
+            s = lo // HALF_G
+            nc.vector.tensor_copy(
+                e_picked[t // 2][s][:, t % 2, lo - s * HALF_G : hi - s * HALF_G],
+                h_plane[t][:].indirect(idx2[:, lo // STRIPE : hi // STRIPE]),
+            )
+
+        def group_e(q, lo, hi):
+            s = lo // HALF_G
+            scalar_copy(
+                e_grouped[:, lo:hi, 2 * q : 2 * q + 2],
+                e_picked[q][s][:, :, lo - s * HALF_G : hi - s * HALF_G].rearrange("p u c -> p c u"),
+            )
+
+        def finish(first, last, empty_bank):
+            lo, hi = STARTS[first], STARTS[last + 1]
+            bank = psum.tile([P, hi - lo], F32, name=f"bank_out{first}")
+            for k in range(first, last + 1):
+                quantize(e_codes[k][:], e_scales[k][:], e_grouped[:, STARTS[k] : STARTS[k + 1], :])
+                columns = bank[:, STARTS[k] - lo : STARTS[k + 1] - lo]
+                multiply(columns, w2_codes[:], w2_scales[:], e_codes[k][:], e_scales[k][:])
+            empty_bank(result[:, lo:hi], bank[:])
+            nc.sync.dma_start(out[:, lo:hi], result[:, lo:hi])
+
+        for s in range(2):
+            for t in range(2):
+                pick(t, s * HALF_G, (s + 1) * HALF_G)
+            group_e(0, s * HALF_G, (s + 1) * HALF_G)
+        for t in range(2, PACK):
+            pick(t, 0, HALF_G)
+        for k in range(2):
+            group_e(1, STARTS[k], STARTS[k + 1])
+        pick(2, HALF_G, G)
+        for k in range(2, len(PARTS)):
+            pick(3, STARTS[k], STARTS[k + 1])
+            group_e(1, STARTS[k], STARTS[k + 1])
+        finish(0, 1, nc.scalar.copy)
+        finish(2, 2, nc.scalar.copy)
+        finish(3, 4, nc.vector.tensor_copy)

@@ -18,10 +18,10 @@ STRIPE = 16
 HALF_N = N // 2
 HALF_H = H // 2
 HALF_M = P // 2
-HALF_G = G // 2
-WINDOW = N + 32
-PARTS = (256, 256, 256, 128, 128)
-STARTS = tuple(sum(PARTS[:k]) for k in range(len(PARTS) + 1))
+PART = 256
+EARLY = 3
+DIRECT = 64
+LATE = G - EARLY * PART - DIRECT
 
 
 def tile_attend_hop_pick_kernel(tc, xT, w1, w2, offs, offs2, out):
@@ -40,36 +40,38 @@ def tile_attend_hop_pick_kernel(tc, xT, w1, w2, offs, offs2, out):
 
         w1_raw = [held.tile([P, PACK, HALF_H], F32, name=f"w1_raw{k}", align_bytes=64) for k in range(2)]
         w1_grouped = held.tile([P, PACK, P, PACK], BF16, align_bytes=64)
-        w1_codes = held.tile([P, PACK, P], U32, align_bytes=64)
+        w1_codes = held.tile([P, PACK, P], U32, align_bytes=64, tag="w1_codes")
         w1_scales = held.tile([P, PACK, P], U8, align_bytes=64)
 
         w2_raw = held.tile([P, PACK, M], F32, align_bytes=64)
-        w2_grouped = held.tile([P, M, PACK], BF16, align_bytes=64)
         w2_codes = held.tile([P, M], U32, align_bytes=64)
         w2_scales = held.tile([P, M], U8, align_bytes=64)
 
-        h_plane = [held.tile([P, WINDOW], F32, name=f"h_plane{t}", align_bytes=64) for t in range(PACK)]
+        h_plane = [held.tile([P, N], F32, name=f"h_plane{t}", align_bytes=64) for t in range(PACK)]
         e_picked = [
-            [held.tile([P, 2, HALF_G], F32, name=f"e_picked{q}{s}", align_bytes=64) for s in range(2)]
+            [held.tile([P, 2, PART], F32, name=f"e_picked{q}{k}", align_bytes=64) for k in range(EARLY)]
             for q in range(2)
         ]
-        e_grouped = held.tile([P, G, PACK], BF16, align_bytes=64)
-        e_codes = [held.tile([P, n], U32, name=f"e_codes{k}", align_bytes=64) for k, n in enumerate(PARTS)]
-        e_scales = [held.tile([P, n], U8, name=f"e_scales{k}", align_bytes=64) for k, n in enumerate(PARTS)]
+        e_grouped = [
+            held.tile([P, PART, PACK], BF16, name=f"e_grouped{k}", tag=f"e_grouped{k}", align_bytes=64)
+            for k in range(EARLY)
+        ]
+        late_grouped = held.tile([P, LATE, PACK], BF16, align_bytes=64)
+        e_codes = [held.tile([P, PART], U32, name=f"e_codes{k}", align_bytes=64) for k in range(EARLY + 1)]
+        e_scales = [held.tile([P, PART], U8, name=f"e_scales{k}", align_bytes=64) for k in range(EARLY + 1)]
         result = held.tile([P, G], F32, align_bytes=64)
 
         x_rows = xT.rearrange("(p t) n -> p t n", t=PACK)
         w1_rows = w1.rearrange("(p j) c -> p j c", j=PACK)
+        nc.sync.dma_start(x_plane[0][:], x_rows[:, 0, :])
         nc.sync.dma_start(idx[:], offs)
-        nc.sync.dma_start(idx2[:], offs2)
-        for t in range(PACK - 1):
+        for t in range(1, PACK - 1):
             nc.sync.dma_start(x_plane[t][:], x_rows[:, t, :])
-        nc.sync.dma_start(w1_raw[0][:], w1_rows[:, :, :HALF_H])
         nc.sync.dma_start(x_plane[PACK - 1][:], x_rows[:, PACK - 1, :])
+        nc.sync.dma_start(w1_raw[0][:], w1_rows[:, :, :HALF_H])
         nc.sync.dma_start(w1_raw[1][:], w1_rows[:, :, HALF_H:])
+        nc.sync.dma_start(idx2[:], offs2)
         nc.sync.dma_start(w2_raw[:], w2.rearrange("(p j) m -> p j m", j=PACK))
-        for t in range(PACK):
-            nc.gpsimd.memset(h_plane[t][:, N:], 0.0)
 
         def scalar_copy(dst, src):
             nc.scalar.activation(dst, src, COPY)
@@ -92,9 +94,9 @@ def tile_attend_hop_pick_kernel(tc, xT, w1, w2, offs, offs2, out):
                 stop=True,
             )
 
-        def group_w1(k, t0, t1):
+        def group_w1(copy, k, t0, t1):
             ms = slice(k * HALF_M, (k + 1) * HALF_M)
-            scalar_copy(
+            copy(
                 w1_grouped[:].rearrange("p t m j -> p m t j")[:, ms, t0:t1, :],
                 w1_raw[k][:].rearrange("p j (m t) -> p m t j", t=PACK)[:, :, t0:t1, :],
             )
@@ -103,17 +105,12 @@ def tile_attend_hop_pick_kernel(tc, xT, w1, w2, offs, offs2, out):
             ms = slice(k * HALF_M, (k + 1) * HALF_M)
             quantize(w1_codes[:, t, ms], w1_scales[:, t, ms], w1_grouped[:, t, ms, :])
 
-        for t in range(PACK - 1):
-            nc.vector.tensor_copy(x_grouped[:, :, t], x_plane[t][:].indirect(idx[:]))
-        group_w1(0, 0, PACK)
-        for t in range(PACK):
-            quantize_w1(t, 0)
-        n_halves = [slice(a * HALF_N, (a + 1) * HALF_N) for a in range(2)]
-        for cols in n_halves:
-            entries = idx[:, cols.start // STRIPE : cols.stop // STRIPE]
-            nc.vector.tensor_copy(x_grouped[:, cols, PACK - 1], x_plane[PACK - 1][:].indirect(entries))
-        group_w1(1, 0, 1)
-        group_w1(1, 1, PACK)
+        def quantize_w1_whole(t0, t1):
+            quantize(
+                w1_codes[:, t0:t1, :].rearrange("p t m -> p (t m)"),
+                w1_scales[:, t0:t1, :].rearrange("p t m -> p (t m)"),
+                w1_grouped[:, t0:t1, :, :].rearrange("p t m j -> p (t m) j"),
+            )
 
         def quantize_x(cols):
             quantize(x_codes[:, cols], x_scales[:, cols], x_grouped[:, cols, :])
@@ -121,60 +118,75 @@ def tile_attend_hop_pick_kernel(tc, xT, w1, w2, offs, offs2, out):
         def first_product(bank, t, cols):
             multiply(bank, w1_codes[:, t, :], w1_scales[:, t, :], x_codes[:, cols], x_scales[:, cols])
 
-        quantize_x(n_halves[0])
+        for t in range(PACK):
+            nc.vector.tensor_copy(x_grouped[:, :, t], x_plane[t][:].indirect(idx[:]))
+        n_halves = [slice(a * HALF_N, (a + 1) * HALF_N) for a in range(2)]
+        group_w1(scalar_copy, 0, 0, 1)
+        group_w1(scalar_copy, 0, 1, PACK)
+        quantize_x(slice(0, N))
+        quantize_w1(0, 0)
+        group_w1(nc.vector.tensor_copy, 1, 0, 1)
+        group_w1(nc.vector.tensor_copy, 1, 1, 2)
+        group_w1(scalar_copy, 1, 2, PACK)
         quantize_w1(0, 1)
-        quantize_x(n_halves[1])
-        bank_halves = [psum.tile([P, HALF_N], F32, name=f"bank_half{a}") for a in range(2)]
+        bank_halves = [psum.tile([P, HALF_N], F32, name=f"bank_half{a}", tag=f"bank_half{a}") for a in range(2)]
         for bank, cols in zip(bank_halves, n_halves):
             first_product(bank[:], 0, cols)
+        quantize_w1_whole(1, 2)
+        quantize_w1_whole(2, PACK)
         nc.scalar.activation(h_plane[0][:, n_halves[0]], bank_halves[0][:], RELU)
-        for t in range(1, PACK):
-            quantize_w1(t, 1)
         nc.vector.tensor_relu(h_plane[0][:, n_halves[1]], bank_halves[1][:])
         for t in range(1, PACK):
             bank = psum.tile([P, N], F32, name=f"bank{t}")
             first_product(bank[:], t, slice(0, N))
             nc.scalar.activation(h_plane[t][:, :N], bank[:], RELU)
 
+        w2_grouped = held.tile([P, M, PACK], BF16, align_bytes=64, tag="w1_codes")
         scalar_copy(w2_grouped[:], w2_raw[:].rearrange("p j m -> p m j"))
         quantize(w2_codes[:], w2_scales[:], w2_grouped[:])
 
-        def pick(t, lo, hi):
-            s = lo // HALF_G
-            nc.vector.tensor_copy(
-                e_picked[t // 2][s][:, t % 2, lo - s * HALF_G : hi - s * HALF_G],
-                h_plane[t][:].indirect(idx2[:, lo // STRIPE : hi // STRIPE]),
-            )
+        def pick(dst, t, lo, hi):
+            nc.vector.tensor_copy(dst, h_plane[t][:].indirect(idx2[:, lo // STRIPE : hi // STRIPE]))
 
-        def group_e(q, lo, hi):
-            s = lo // HALF_G
-            scalar_copy(
-                e_grouped[:, lo:hi, 2 * q : 2 * q + 2],
-                e_picked[q][s][:, :, lo - s * HALF_G : hi - s * HALF_G].rearrange("p u c -> p c u"),
-            )
+        def second_product(bank, k, cols=slice(0, PART)):
+            multiply(bank, w2_codes[:], w2_scales[:], e_codes[k][:, cols], e_scales[k][:, cols])
 
-        def finish(first, last, empty_bank):
-            lo, hi = STARTS[first], STARTS[last + 1]
-            bank = psum.tile([P, hi - lo], F32, name=f"bank_out{first}")
-            for k in range(first, last + 1):
-                quantize(e_codes[k][:], e_scales[k][:], e_grouped[:, STARTS[k] : STARTS[k + 1], :])
-                columns = bank[:, STARTS[k] - lo : STARTS[k + 1] - lo]
-                multiply(columns, w2_codes[:], w2_scales[:], e_codes[k][:], e_scales[k][:])
-            empty_bank(result[:, lo:hi], bank[:])
+        def store(lo, hi, bank, empty_bank):
+            empty_bank(result[:, lo:hi], bank)
             nc.sync.dma_start(out[:, lo:hi], result[:, lo:hi])
 
-        for s in range(2):
-            for t in range(2):
-                pick(t, s * HALF_G, (s + 1) * HALF_G)
-            group_e(0, s * HALF_G, (s + 1) * HALF_G)
-        for t in range(2, PACK):
-            pick(t, 0, HALF_G)
-        for k in range(2):
-            group_e(1, STARTS[k], STARTS[k + 1])
-        pick(2, HALF_G, G)
-        for k in range(2, len(PARTS)):
-            pick(3, STARTS[k], STARTS[k + 1])
-            group_e(1, STARTS[k], STARTS[k + 1])
-        finish(0, 1, nc.scalar.copy)
-        finish(2, 2, nc.scalar.copy)
-        finish(3, 4, nc.vector.tensor_copy)
+        for q in range(2):
+            for k in range(EARLY):
+                for u in range(2):
+                    pick(e_picked[q][k][:, u, :], 2 * q + u, k * PART, (k + 1) * PART)
+                scalar_copy(e_grouped[k][:, :, 2 * q : 2 * q + 2], e_picked[q][k][:].rearrange("p u c -> p c u"))
+        quantize(e_codes[0][:], e_scales[0][:], e_grouped[0][:])
+
+        late_lo = EARLY * PART
+        late_picked = held.tile([P, PACK, LATE], F32, tag="e_grouped0", align_bytes=64)
+        for t in range(PACK):
+            pick(late_picked[:, t, :], t, late_lo, late_lo + LATE)
+        scalar_copy(late_grouped[:], late_picked[:].rearrange("p t c -> p c t"))
+        bank0 = psum.tile([P, PART], F32)
+        second_product(bank0[:], 0)
+        store(0, PART, bank0[:], nc.scalar.copy)
+
+        bank12 = psum.tile([P, 2 * PART], F32)
+        for k in range(1, EARLY):
+            quantize(e_codes[k][:], e_scales[k][:], e_grouped[k][:])
+            second_product(bank12[:, (k - 1) * PART : k * PART], k)
+        store(PART, EARLY * PART, bank12[:], nc.scalar.copy)
+
+        direct_grouped = held.tile([P, DIRECT, PACK], BF16, tag=f"e_grouped{EARLY - 1}", align_bytes=64)
+        for t in range(PACK):
+            pick(direct_grouped[:, :, t], t, G - DIRECT, G)
+        codes, scales = e_codes[EARLY], e_scales[EARLY]
+        bank_late = psum.tile([P, LATE], F32, tag="bank_half0")
+        bank_direct = psum.tile([P, DIRECT], F32, tag="bank_half1")
+        for cols in (slice(0, 128), slice(128, LATE)):
+            quantize(codes[:, cols], scales[:, cols], late_grouped[:, cols, :])
+            second_product(bank_late[:, cols], EARLY, cols)
+        quantize(codes[:, LATE:], scales[:, LATE:], direct_grouped[:])
+        second_product(bank_direct[:], EARLY, slice(LATE, PART))
+        store(late_lo, late_lo + LATE, bank_late[:], nc.scalar.copy)
+        store(G - DIRECT, G, bank_direct[:], nc.vector.tensor_copy)

@@ -9,19 +9,26 @@ U32 = mybir.dt.uint32
 U16 = mybir.dt.uint16
 U8 = mybir.dt.uint8
 FP8X4 = mybir.dt.float8_e4m3fn_x4
-COPY = mybir.ActivationFunctionType.Copy
 RELU = mybir.ActivationFunctionType.Relu
 
 P = 128
 PACK = 4
 STRIPE = 16
+LINE = 4
 HALF_N = N // 2
-HALF_H = H // 2
-HALF_M = P // 2
-PART = 256
-EARLY = 3
-DIRECT = 64
-LATE = G - EARLY * PART - DIRECT
+PARTS = (384, 256, 192, 128, 64)
+STARTS = tuple(sum(PARTS[:k]) for k in range(len(PARTS) + 1))
+LAST = len(PARTS) - 1
+WIDTHS = (256, 128, 64)
+
+
+def cut(n):
+    pieces, lo = [], 0
+    for width in WIDTHS:
+        while n - lo >= width:
+            pieces.append(slice(lo, lo + width))
+            lo += width
+    return pieces
 
 
 def tile_attend_hop_pick_kernel(tc, xT, w1, w2, offs, offs2, out):
@@ -35,46 +42,30 @@ def tile_attend_hop_pick_kernel(tc, xT, w1, w2, offs, offs2, out):
 
         x_plane = [held.tile([P, T], F32, name=f"x_plane{t}", align_bytes=64) for t in range(PACK)]
         x_grouped = held.tile([P, N, PACK], BF16, align_bytes=64)
-        x_codes = held.tile([P, N], U32, align_bytes=64)
+        x_codes = held.tile([P, N], U32, align_bytes=64, tag="x_codes")
         x_scales = held.tile([P, N], U8, align_bytes=64)
 
-        w1_raw = [held.tile([P, PACK, HALF_H], F32, name=f"w1_raw{k}", align_bytes=64) for k in range(2)]
-        w1_grouped = held.tile([P, PACK, P, PACK], BF16, align_bytes=64)
-        w1_codes = held.tile([P, PACK, P], U32, align_bytes=64, tag="w1_codes")
+        w1_raw = [held.tile([P, 2, H], F32, name=f"w1_raw{k}", align_bytes=64) for k in range(2)]
+        w1_grouped = [held.tile([P, 2, P, PACK], BF16, name=f"w1_grouped{q}", align_bytes=64) for q in range(2)]
         w1_scales = held.tile([P, PACK, P], U8, align_bytes=64)
 
-        w2_raw = held.tile([P, PACK, M], F32, align_bytes=64)
+        w2_raw = held.tile([P, PACK, M], F32, align_bytes=64, tag="picked1")
         w2_codes = held.tile([P, M], U32, align_bytes=64)
         w2_scales = held.tile([P, M], U8, align_bytes=64)
 
         h_plane = [held.tile([P, N], F32, name=f"h_plane{t}", align_bytes=64) for t in range(PACK)]
-        e_picked = [
-            [held.tile([P, 2, PART], F32, name=f"e_picked{q}{k}", align_bytes=64) for k in range(EARLY)]
-            for q in range(2)
-        ]
-        e_grouped = [
-            held.tile([P, PART, PACK], BF16, name=f"e_grouped{k}", tag=f"e_grouped{k}", align_bytes=64)
-            for k in range(EARLY)
-        ]
-        late_grouped = held.tile([P, LATE, PACK], BF16, align_bytes=64)
-        e_codes = [held.tile([P, PART], U32, name=f"e_codes{k}", align_bytes=64) for k in range(EARLY + 1)]
-        e_scales = [held.tile([P, PART], U8, name=f"e_scales{k}", align_bytes=64) for k in range(EARLY + 1)]
         result = held.tile([P, G], F32, align_bytes=64)
 
         x_rows = xT.rearrange("(p t) n -> p t n", t=PACK)
         w1_rows = w1.rearrange("(p j) c -> p j c", j=PACK)
         nc.sync.dma_start(x_plane[0][:], x_rows[:, 0, :])
         nc.sync.dma_start(idx[:], offs)
-        for t in range(1, PACK - 1):
+        for t in range(1, PACK):
             nc.sync.dma_start(x_plane[t][:], x_rows[:, t, :])
-        nc.sync.dma_start(x_plane[PACK - 1][:], x_rows[:, PACK - 1, :])
-        nc.sync.dma_start(w1_raw[0][:], w1_rows[:, :, :HALF_H])
-        nc.sync.dma_start(w1_raw[1][:], w1_rows[:, :, HALF_H:])
+        for k in range(2):
+            nc.sync.dma_start(w1_raw[k][:], w1_rows[:, 2 * k : 2 * k + 2, :])
         nc.sync.dma_start(idx2[:], offs2)
         nc.sync.dma_start(w2_raw[:], w2.rearrange("(p j) m -> p j m", j=PACK))
-
-        def scalar_copy(dst, src):
-            nc.scalar.activation(dst, src, COPY)
 
         def quantize(codes, scales, grouped):
             nc.vector.quantize_mx(
@@ -94,99 +85,93 @@ def tile_attend_hop_pick_kernel(tc, xT, w1, w2, offs, offs2, out):
                 stop=True,
             )
 
-        def group_w1(copy, k, t0, t1):
-            ms = slice(k * HALF_M, (k + 1) * HALF_M)
+        def interleave(grouped, planes):
+            nc.scalar.copy(
+                grouped.rearrange("p (c i) t -> p c t i", i=LINE),
+                planes.rearrange("p t (c i) -> p c t i", i=LINE),
+            )
+
+        def group_w1(copy, k, q):
             copy(
-                w1_grouped[:].rearrange("p t m j -> p m t j")[:, ms, t0:t1, :],
-                w1_raw[k][:].rearrange("p j (m t) -> p m t j", t=PACK)[:, :, t0:t1, :],
+                w1_grouped[q][:, :, :, 2 * k : 2 * k + 2].rearrange("p v m u -> p m u v"),
+                w1_raw[k][:].rearrange("p u (m t) -> p m u t", t=PACK)[:, :, :, 2 * q : 2 * q + 2],
             )
 
-        def quantize_w1(t, k):
-            ms = slice(k * HALF_M, (k + 1) * HALF_M)
-            quantize(w1_codes[:, t, ms], w1_scales[:, t, ms], w1_grouped[:, t, ms, :])
+        def quantize_w1(t, tag):
+            codes = held.tile([P, P], U32, name=f"w1_codes{t}", tag=tag, align_bytes=64)
+            quantize(codes[:], w1_scales[:, t, :], w1_grouped[t // 2][:, t % 2, :, :])
+            return codes
 
-        def quantize_w1_whole(t0, t1):
-            quantize(
-                w1_codes[:, t0:t1, :].rearrange("p t m -> p (t m)"),
-                w1_scales[:, t0:t1, :].rearrange("p t m -> p (t m)"),
-                w1_grouped[:, t0:t1, :, :].rearrange("p t m j -> p (t m) j"),
-            )
+        def first_product(bank, t, codes, cols):
+            multiply(bank, codes[:], w1_scales[:, t, :], x_codes[:, cols], x_scales[:, cols])
 
-        def quantize_x(cols):
-            quantize(x_codes[:, cols], x_scales[:, cols], x_grouped[:, cols, :])
-
-        def first_product(bank, t, cols):
-            multiply(bank, w1_codes[:, t, :], w1_scales[:, t, :], x_codes[:, cols], x_scales[:, cols])
-
-        for t in range(PACK):
+        for t in range(PACK - 1):
             nc.vector.tensor_copy(x_grouped[:, :, t], x_plane[t][:].indirect(idx[:]))
         n_halves = [slice(a * HALF_N, (a + 1) * HALF_N) for a in range(2)]
-        group_w1(scalar_copy, 0, 0, 1)
-        group_w1(scalar_copy, 0, 1, PACK)
-        quantize_x(slice(0, N))
-        quantize_w1(0, 0)
-        group_w1(nc.vector.tensor_copy, 1, 0, 1)
-        group_w1(nc.vector.tensor_copy, 1, 1, 2)
-        group_w1(scalar_copy, 1, 2, PACK)
-        quantize_w1(0, 1)
+        for cols in n_halves:
+            entries = idx[:, cols.start // STRIPE : cols.stop // STRIPE]
+            nc.vector.tensor_copy(x_grouped[:, cols, PACK - 1], x_plane[PACK - 1][:].indirect(entries))
+        for cols in n_halves:
+            quantize(x_codes[:, cols], x_scales[:, cols], x_grouped[:, cols, :])
+        group_w1(nc.scalar.copy, 0, 0)
+        group_w1(nc.scalar.copy, 0, 1)
+        group_w1(nc.vector.tensor_copy, 1, 0)
+        group_w1(nc.scalar.copy, 1, 1)
+
+        codes0 = quantize_w1(0, "w1_codes0")
         bank_halves = [psum.tile([P, HALF_N], F32, name=f"bank_half{a}", tag=f"bank_half{a}") for a in range(2)]
         for bank, cols in zip(bank_halves, n_halves):
-            first_product(bank[:], 0, cols)
-        quantize_w1_whole(1, 2)
-        quantize_w1_whole(2, PACK)
+            first_product(bank[:], 0, codes0, cols)
+        codes = [codes0, quantize_w1(1, "w1_codes1"), quantize_w1(2, "w1_codes2")]
         nc.scalar.activation(h_plane[0][:, n_halves[0]], bank_halves[0][:], RELU)
         nc.vector.tensor_relu(h_plane[0][:, n_halves[1]], bank_halves[1][:])
+        codes.append(quantize_w1(3, "w1_codes0"))
         for t in range(1, PACK):
-            bank = psum.tile([P, N], F32, name=f"bank{t}")
-            first_product(bank[:], t, slice(0, N))
-            nc.scalar.activation(h_plane[t][:, :N], bank[:], RELU)
+            bank = psum.tile([P, N], F32, name=f"bank{t}", tag=f"bank{t}")
+            first_product(bank[:], t, codes[t], slice(0, N))
+            nc.scalar.activation(h_plane[t][:], bank[:], RELU)
 
-        w2_grouped = held.tile([P, M, PACK], BF16, align_bytes=64, tag="w1_codes")
-        scalar_copy(w2_grouped[:], w2_raw[:].rearrange("p j m -> p m j"))
+        w2_grouped = held.tile([P, M, PACK], BF16, align_bytes=64, tag="x_codes")
+        interleave(w2_grouped[:], w2_raw[:])
         quantize(w2_codes[:], w2_scales[:], w2_grouped[:])
 
-        def pick(dst, t, lo, hi):
-            nc.vector.tensor_copy(dst, h_plane[t][:].indirect(idx2[:, lo // STRIPE : hi // STRIPE]))
+        def pick(dst, t, k):
+            entries = idx2[:, STARTS[k] // STRIPE : STARTS[k + 1] // STRIPE]
+            nc.vector.tensor_copy(dst, h_plane[t][:].indirect(entries))
 
-        def second_product(bank, k, cols=slice(0, PART)):
-            multiply(bank, w2_codes[:], w2_scales[:], e_codes[k][:, cols], e_scales[k][:, cols])
+        def gather_part(k):
+            place = f"picked{k % 2}"
+            if k == LAST:
+                grouped = held.tile([P, PARTS[k], PACK], BF16, name=f"e_grouped{k}", tag=place, align_bytes=64)
+                for t in range(PACK):
+                    pick(grouped[:, :, t], t, k)
+                return grouped
+            picked = held.tile([P, PACK, PARTS[k]], F32, name=f"e_picked{k}", tag=place, align_bytes=64)
+            grouped = held.tile([P, PARTS[k], PACK], BF16, name=f"e_grouped{k}", align_bytes=64)
+            for t in range(PACK):
+                pick(picked[:, t, :], t, k)
+            interleave(grouped[:], picked[:])
+            return grouped
 
-        def store(lo, hi, bank, empty_bank):
-            empty_bank(result[:, lo:hi], bank)
-            nc.sync.dma_start(out[:, lo:hi], result[:, lo:hi])
+        def finish_part(k, grouped, tag, bank_tag, empty_bank):
+            e_codes = held.tile([P, PARTS[k]], U32, name=f"e_codes{k}", tag=tag, align_bytes=64)
+            e_scales = held.tile([P, PARTS[k]], U8, name=f"e_scales{k}", align_bytes=64)
+            bank = psum.tile([P, PARTS[k]], F32, name=f"bank_out{k}", tag=bank_tag)
+            for cols in cut(PARTS[k]):
+                quantize(e_codes[:, cols], e_scales[:, cols], grouped[:, cols, :])
+                multiply(bank[:, cols], w2_codes[:], w2_scales[:], e_codes[:, cols], e_scales[:, cols])
+            empty_bank(result[:, STARTS[k] : STARTS[k + 1]], bank[:])
 
-        for q in range(2):
-            for k in range(EARLY):
-                for u in range(2):
-                    pick(e_picked[q][k][:, u, :], 2 * q + u, k * PART, (k + 1) * PART)
-                scalar_copy(e_grouped[k][:, :, 2 * q : 2 * q + 2], e_picked[q][k][:].rearrange("p u c -> p c u"))
-        quantize(e_codes[0][:], e_scales[0][:], e_grouped[0][:])
+        def store(first, last):
+            cols = slice(STARTS[first], STARTS[last + 1])
+            nc.sync.dma_start(out[:, cols], result[:, cols])
 
-        late_lo = EARLY * PART
-        late_picked = held.tile([P, PACK, LATE], F32, tag="e_grouped0", align_bytes=64)
-        for t in range(PACK):
-            pick(late_picked[:, t, :], t, late_lo, late_lo + LATE)
-        scalar_copy(late_grouped[:], late_picked[:].rearrange("p t c -> p c t"))
-        bank0 = psum.tile([P, PART], F32)
-        second_product(bank0[:], 0)
-        store(0, PART, bank0[:], nc.scalar.copy)
-
-        bank12 = psum.tile([P, 2 * PART], F32)
-        for k in range(1, EARLY):
-            quantize(e_codes[k][:], e_scales[k][:], e_grouped[k][:])
-            second_product(bank12[:, (k - 1) * PART : k * PART], k)
-        store(PART, EARLY * PART, bank12[:], nc.scalar.copy)
-
-        direct_grouped = held.tile([P, DIRECT, PACK], BF16, tag=f"e_grouped{EARLY - 1}", align_bytes=64)
-        for t in range(PACK):
-            pick(direct_grouped[:, :, t], t, G - DIRECT, G)
-        codes, scales = e_codes[EARLY], e_scales[EARLY]
-        bank_late = psum.tile([P, LATE], F32, tag="bank_half0")
-        bank_direct = psum.tile([P, DIRECT], F32, tag="bank_half1")
-        for cols in (slice(0, 128), slice(128, LATE)):
-            quantize(codes[:, cols], scales[:, cols], late_grouped[:, cols, :])
-            second_product(bank_late[:, cols], EARLY, cols)
-        quantize(codes[:, LATE:], scales[:, LATE:], direct_grouped[:])
-        second_product(bank_direct[:], EARLY, slice(LATE, PART))
-        store(late_lo, late_lo + LATE, bank_late[:], nc.scalar.copy)
-        store(G - DIRECT, G, bank_direct[:], nc.vector.tensor_copy)
+        grouped = gather_part(0)
+        for k in range(LAST):
+            following = gather_part(k + 1)
+            finish_part(k, grouped, f"e_codes{k}", f"bank_out{k}" if k < 3 else "bank_half0", nc.scalar.copy)
+            if k < LAST - 1:
+                store(k, k)
+            grouped = following
+        finish_part(LAST, grouped, f"picked{(LAST - 1) % 2}", "bank_half1", nc.vector.tensor_copy)
+        store(LAST - 1, LAST)

@@ -16,7 +16,7 @@ PACK = 4
 STRIPE = 16
 LINE = 4
 HALF_N = N // 2
-PARTS = (384, 256, 192, 128, 64)
+PARTS = (448, 320, 128, 128)
 STARTS = tuple(sum(PARTS[:k]) for k in range(len(PARTS) + 1))
 LAST = len(PARTS) - 1
 WIDTHS = (256, 128, 64)
@@ -119,12 +119,17 @@ def tile_attend_hop_pick_kernel(tc, xT, w1, w2, offs, offs2, out):
         group_w1(nc.scalar.copy, 1, 1)
 
         codes0 = quantize_w1(0, "w1_codes0")
-        bank_halves = [psum.tile([P, HALF_N], F32, name=f"bank_half{a}", tag=f"bank_half{a}") for a in range(2)]
-        for bank, cols in zip(bank_halves, n_halves):
+        pieces = (slice(0, HALF_N), slice(HALF_N, 3 * N // 4), slice(3 * N // 4, N))
+        banks = [
+            psum.tile([P, cols.stop - cols.start], F32, name=f"bank_piece{a}", tag=f"bank_piece{a}")
+            for a, cols in enumerate(pieces)
+        ]
+        for bank, cols in zip(banks, pieces):
             first_product(bank[:], 0, codes0, cols)
         codes = [codes0, quantize_w1(1, "w1_codes1"), quantize_w1(2, "w1_codes2")]
-        nc.scalar.activation(h_plane[0][:, n_halves[0]], bank_halves[0][:], RELU)
-        nc.vector.tensor_relu(h_plane[0][:, n_halves[1]], bank_halves[1][:])
+        nc.vector.tensor_relu(h_plane[0][:, pieces[0]], banks[0][:])
+        for bank, cols in zip(banks[1:], pieces[1:]):
+            nc.scalar.activation(h_plane[0][:, cols], bank[:], RELU)
         codes.append(quantize_w1(3, "w1_codes0"))
         for t in range(1, PACK):
             bank = psum.tile([P, N], F32, name=f"bank{t}", tag=f"bank{t}")
@@ -135,21 +140,18 @@ def tile_attend_hop_pick_kernel(tc, xT, w1, w2, offs, offs2, out):
         interleave(w2_grouped[:], w2_raw[:])
         quantize(w2_codes[:], w2_scales[:], w2_grouped[:])
 
-        def pick(dst, t, k):
-            entries = idx2[:, STARTS[k] // STRIPE : STARTS[k + 1] // STRIPE]
-            nc.vector.tensor_copy(dst, h_plane[t][:].indirect(entries))
+        def pick(dst, t, lo, hi):
+            nc.vector.tensor_copy(dst, h_plane[t][:].indirect(idx2[:, lo // STRIPE : hi // STRIPE]))
+
+        def place(k):
+            return f"picked{k % 2}"
 
         def gather_part(k):
-            place = f"picked{k % 2}"
-            if k == LAST:
-                grouped = held.tile([P, PARTS[k], PACK], BF16, name=f"e_grouped{k}", tag=place, align_bytes=64)
-                for t in range(PACK):
-                    pick(grouped[:, :, t], t, k)
-                return grouped
-            picked = held.tile([P, PACK, PARTS[k]], F32, name=f"e_picked{k}", tag=place, align_bytes=64)
-            grouped = held.tile([P, PARTS[k], PACK], BF16, name=f"e_grouped{k}", align_bytes=64)
+            lo, hi = STARTS[k], STARTS[k + 1]
+            picked = held.tile([P, PACK, hi - lo], F32, name=f"e_picked{k}", tag=place(k), align_bytes=64)
+            grouped = held.tile([P, hi - lo, PACK], BF16, name=f"e_grouped{k}", align_bytes=64)
             for t in range(PACK):
-                pick(picked[:, t, :], t, k)
+                pick(picked[:, t, :], t, lo, hi)
             interleave(grouped[:], picked[:])
             return grouped
 
@@ -162,16 +164,30 @@ def tile_attend_hop_pick_kernel(tc, xT, w1, w2, offs, offs2, out):
                 multiply(bank[:, cols], w2_codes[:], w2_scales[:], e_codes[:, cols], e_scales[:, cols])
             empty_bank(result[:, STARTS[k] : STARTS[k + 1]], bank[:])
 
-        def store(first, last):
-            cols = slice(STARTS[first], STARTS[last + 1])
-            nc.sync.dma_start(out[:, cols], result[:, cols])
+        def store(k, queue):
+            cols = slice(STARTS[k], STARTS[k + 1])
+            queue.dma_start(out[:, cols], result[:, cols])
 
-        grouped = gather_part(0)
-        for k in range(LAST):
-            following = gather_part(k + 1)
-            finish_part(k, grouped, f"e_codes{k}", f"bank_out{k}" if k < 3 else "bank_half0", nc.scalar.copy)
-            if k < LAST - 1:
-                store(k, k)
-            grouped = following
-        finish_part(LAST, grouped, f"picked{(LAST - 1) % 2}", "bank_half1", nc.vector.tensor_copy)
-        store(LAST - 1, LAST)
+        first = gather_part(0)
+        second = gather_part(1)
+        finish_part(0, first, "e_codes0", "bank_out0", nc.scalar.copy)
+        store(0, nc.sync)
+
+        width = PARTS[2]
+        picked = held.tile([P, PACK, G - STARTS[2]], F32, tag=place(2), align_bytes=64)
+        third = held.tile([P, width, PACK], BF16, align_bytes=64)
+        last = held.tile([P, PARTS[LAST], PACK], BF16, tag=place(LAST), align_bytes=64)
+        for t in range(PACK):
+            hi = G if t < 2 else STARTS[LAST]
+            pick(picked[:, t, : hi - STARTS[2]], t, STARTS[2], hi)
+        nc.scalar.copy(last[:, :, :2], picked[:, :2, width:].rearrange("p u c -> p c u"))
+        interleave(third[:], picked[:, :, :width])
+        finish_part(1, second, "e_codes1", "bank_out1", nc.scalar.copy)
+        store(1, nc.sync)
+
+        for t in range(2, PACK):
+            pick(last[:, :, t], t, STARTS[LAST], G)
+        finish_part(2, third, "e_codes2", "bank_piece0", nc.scalar.copy)
+        store(2, nc.scalar)
+        finish_part(LAST, last, place(2), "bank_piece1", nc.vector.tensor_copy)
+        store(LAST, nc.sync)

@@ -45,7 +45,7 @@ def tile_attend_hop_pick_kernel(tc, xT, w1, w2, offs, offs2, out):
         x_codes = held.tile([P, N], U32, align_bytes=64, tag="x_codes")
         x_scales = held.tile([P, N], U8, align_bytes=64)
 
-        w1_raw = [held.tile([P, 2, H], F32, name=f"w1_raw{k}", align_bytes=64) for k in range(2)]
+        w1_raw = held.tile([P, PACK, H], F32, align_bytes=64)
         w1_grouped = [held.tile([P, 2, P, PACK], BF16, name=f"w1_grouped{q}", align_bytes=64) for q in range(2)]
         w1_scales = held.tile([P, PACK, P], U8, align_bytes=64)
 
@@ -63,7 +63,7 @@ def tile_attend_hop_pick_kernel(tc, xT, w1, w2, offs, offs2, out):
         for t in range(1, PACK):
             nc.sync.dma_start(x_plane[t][:], x_rows[:, t, :])
         for k in range(2):
-            nc.sync.dma_start(w1_raw[k][:], w1_rows[:, 2 * k : 2 * k + 2, :])
+            nc.sync.dma_start(w1_raw[:, 2 * k : 2 * k + 2, :], w1_rows[:, 2 * k : 2 * k + 2, :])
         nc.sync.dma_start(idx2[:], offs2)
         nc.sync.dma_start(w2_raw[:], w2.rearrange("(p j) m -> p j m", j=PACK))
 
@@ -91,19 +91,24 @@ def tile_attend_hop_pick_kernel(tc, xT, w1, w2, offs, offs2, out):
                 planes.rearrange("p t (c i) -> p c t i", i=LINE),
             )
 
-        def group_w1(copy, k, q):
+        def group_w1(copy, rows, q):
             copy(
-                w1_grouped[q][:, :, :, 2 * k : 2 * k + 2].rearrange("p v m u -> p m u v"),
-                w1_raw[k][:].rearrange("p u (m t) -> p m u t", t=PACK)[:, :, :, 2 * q : 2 * q + 2],
+                w1_grouped[q][:, :, :, rows].rearrange("p v m j -> p m j v"),
+                w1_raw[:, rows, :].rearrange("p j (m t) -> p m j t", t=PACK)[:, :, :, 2 * q : 2 * q + 2],
             )
 
-        def quantize_w1(t, tag):
-            codes = held.tile([P, P], U32, name=f"w1_codes{t}", tag=tag, align_bytes=64)
-            quantize(codes[:], w1_scales[:, t, :], w1_grouped[t // 2][:, t % 2, :, :])
-            return codes
+        def quantize_w1(t0, t1, tag):
+            q = t0 // 2
+            codes = held.tile([P, t1 - t0, P], U32, name=f"w1_codes{t0}", tag=tag, align_bytes=64)
+            quantize(
+                codes[:].rearrange("p t m -> p (t m)"),
+                w1_scales[:, t0:t1, :].rearrange("p t m -> p (t m)"),
+                w1_grouped[q][:, t0 - 2 * q : t1 - 2 * q, :, :].rearrange("p t m j -> p (t m) j"),
+            )
+            return [codes[:, t, :] for t in range(t1 - t0)]
 
         def first_product(bank, t, codes, cols):
-            multiply(bank, codes[:], w1_scales[:, t, :], x_codes[:, cols], x_scales[:, cols])
+            multiply(bank, codes, w1_scales[:, t, :], x_codes[:, cols], x_scales[:, cols])
 
         for t in range(PACK - 1):
             nc.vector.tensor_copy(x_grouped[:, :, t], x_plane[t][:].indirect(idx[:]))
@@ -113,24 +118,23 @@ def tile_attend_hop_pick_kernel(tc, xT, w1, w2, offs, offs2, out):
             nc.vector.tensor_copy(x_grouped[:, cols, PACK - 1], x_plane[PACK - 1][:].indirect(entries))
         for cols in n_halves:
             quantize(x_codes[:, cols], x_scales[:, cols], x_grouped[:, cols, :])
-        group_w1(nc.scalar.copy, 0, 0)
-        group_w1(nc.scalar.copy, 0, 1)
-        group_w1(nc.vector.tensor_copy, 1, 0)
-        group_w1(nc.scalar.copy, 1, 1)
+        group_w1(nc.scalar.copy, slice(0, 2), 0)
+        group_w1(nc.vector.tensor_copy, slice(2, PACK), 0)
+        group_w1(nc.scalar.copy, slice(0, PACK), 1)
 
-        codes0 = quantize_w1(0, "w1_codes0")
+        codes = quantize_w1(0, 1, "w1_codes0")
         pieces = (slice(0, HALF_N), slice(HALF_N, 3 * N // 4), slice(3 * N // 4, N))
         banks = [
             psum.tile([P, cols.stop - cols.start], F32, name=f"bank_piece{a}", tag=f"bank_piece{a}")
             for a, cols in enumerate(pieces)
         ]
         for bank, cols in zip(banks, pieces):
-            first_product(bank[:], 0, codes0, cols)
-        codes = [codes0, quantize_w1(1, "w1_codes1"), quantize_w1(2, "w1_codes2")]
+            first_product(bank[:], 0, codes[0], cols)
+        codes.extend(quantize_w1(1, 2, "w1_codes1"))
         nc.vector.tensor_relu(h_plane[0][:, pieces[0]], banks[0][:])
         for bank, cols in zip(banks[1:], pieces[1:]):
             nc.scalar.activation(h_plane[0][:, cols], bank[:], RELU)
-        codes.append(quantize_w1(3, "w1_codes0"))
+        codes.extend(quantize_w1(2, PACK, "w1_codes0"))
         for t in range(1, PACK):
             bank = psum.tile([P, N], F32, name=f"bank{t}", tag=f"bank{t}")
             first_product(bank[:], t, codes[t], slice(0, N))

@@ -16,7 +16,7 @@ PACK = 4
 STRIPE = 16
 LINE = 4
 HALF_N = N // 2
-PARTS = (448, 320, 128, 128)
+PARTS = (384, 384, 192, 64)
 STARTS = tuple(sum(PARTS[:k]) for k in range(len(PARTS) + 1))
 LAST = len(PARTS) - 1
 WIDTHS = (256, 128, 64)
@@ -49,11 +49,12 @@ def tile_attend_hop_pick_kernel(tc, xT, w1, w2, offs, offs2, out):
         w1_grouped = [held.tile([P, 2, P, PACK], BF16, name=f"w1_grouped{q}", align_bytes=64) for q in range(2)]
         w1_scales = held.tile([P, PACK, P], U8, align_bytes=64)
 
-        w2_raw = held.tile([P, PACK, M], F32, align_bytes=64, tag="picked1")
+        w2_raw = held.tile([P, PACK, M], F32, align_bytes=64)
         w2_codes = held.tile([P, M], U32, align_bytes=64)
         w2_scales = held.tile([P, M], U8, align_bytes=64)
 
-        h_plane = [held.tile([P, N], F32, name=f"h_plane{t}", align_bytes=64) for t in range(PACK)]
+        h_all = held.tile([P, PACK * N], F32, align_bytes=64)
+        h_plane = [h_all[:, t * N : (t + 1) * N] for t in range(PACK)]
         result = held.tile([P, G], F32, align_bytes=64)
 
         x_rows = xT.rearrange("(p t) n -> p t n", t=PACK)
@@ -86,7 +87,7 @@ def tile_attend_hop_pick_kernel(tc, xT, w1, w2, offs, offs2, out):
             )
 
         def interleave(grouped, planes):
-            nc.scalar.copy(
+            nc.vector.tensor_copy(
                 grouped.rearrange("p (c i) t -> p c t i", i=LINE),
                 planes.rearrange("p t (c i) -> p c t i", i=LINE),
             )
@@ -123,40 +124,39 @@ def tile_attend_hop_pick_kernel(tc, xT, w1, w2, offs, offs2, out):
         group_w1(nc.scalar.copy, slice(0, PACK), 1)
 
         codes = quantize_w1(0, 1, "w1_codes0")
-        pieces = (slice(0, HALF_N), slice(HALF_N, 3 * N // 4), slice(3 * N // 4, N))
-        banks = [
-            psum.tile([P, cols.stop - cols.start], F32, name=f"bank_piece{a}", tag=f"bank_piece{a}")
-            for a, cols in enumerate(pieces)
-        ]
-        for bank, cols in zip(banks, pieces):
+        for a in range(PACK):
+            cols = slice(a * P, (a + 1) * P)
+            bank = psum.tile([P, P], F32, name=f"bank_piece{a}", tag=f"bank_piece{a}")
             first_product(bank[:], 0, codes[0], cols)
-        codes.extend(quantize_w1(1, 2, "w1_codes1"))
-        nc.vector.tensor_relu(h_plane[0][:, pieces[0]], banks[0][:])
-        for bank, cols in zip(banks[1:], pieces[1:]):
             nc.scalar.activation(h_plane[0][:, cols], bank[:], RELU)
-        codes.extend(quantize_w1(2, PACK, "w1_codes0"))
+        codes.extend(quantize_w1(1, 2, "w1_codes1"))
+        w2_grouped = held.tile([P, M, PACK], BF16, align_bytes=64)
+        interleave(w2_grouped[:], w2_raw[:])
+        codes.extend(quantize_w1(2, PACK, "w1_codes2"))
+        quantize(w2_codes[:], w2_scales[:], w2_grouped[:])
         for t in range(1, PACK):
             bank = psum.tile([P, N], F32, name=f"bank{t}", tag=f"bank{t}")
             first_product(bank[:], t, codes[t], slice(0, N))
-            nc.scalar.activation(h_plane[t][:], bank[:], RELU)
+            nc.scalar.activation(h_plane[t], bank[:], RELU)
 
-        w2_grouped = held.tile([P, M, PACK], BF16, align_bytes=64, tag="x_codes")
-        interleave(w2_grouped[:], w2_raw[:])
-        quantize(w2_codes[:], w2_scales[:], w2_grouped[:])
+        def pick(dst, t, lo, hi, planes=1):
+            nc.vector.tensor_copy(dst, h_all[:, t * N : (t + planes) * N].indirect(idx2[:, lo // STRIPE : hi // STRIPE]))
 
-        def pick(dst, t, lo, hi):
-            nc.vector.tensor_copy(dst, h_plane[t][:].indirect(idx2[:, lo // STRIPE : hi // STRIPE]))
+        def words(tile):
+            per_column = tile.shape[2] // 2
+            flat = tile.rearrange("p c t -> p (c t)").bitcast(U32)
+            return flat.rearrange("p (c u) -> p c u", u=per_column)
 
         def place(k):
-            return f"picked{k % 2}"
+            return f"paired{k % 2}"
 
-        def gather_part(k):
-            lo, hi = STARTS[k], STARTS[k + 1]
-            picked = held.tile([P, PACK, hi - lo], F32, name=f"e_picked{k}", tag=place(k), align_bytes=64)
-            grouped = held.tile([P, hi - lo, PACK], BF16, name=f"e_grouped{k}", align_bytes=64)
-            for t in range(PACK):
-                pick(picked[:, t, :], t, lo, hi)
-            interleave(grouped[:], picked[:])
+        def new_pairs(k, width):
+            return held.tile([P, 2, width, 2], BF16, name=f"e_pairs{k}", tag=place(k), align_bytes=64)
+
+        def weave(k, pairs):
+            grouped = held.tile([P, PARTS[k], PACK], BF16, name=f"e_grouped{k}", align_bytes=64)
+            both = pairs[:].rearrange("p u c v -> p (u c v)").bitcast(U32).rearrange("p (u c) -> p c u", u=2)
+            nc.scalar.copy(words(grouped[:]), both[:, : PARTS[k], :])
             return grouped
 
         def finish_part(k, grouped, tag, bank_tag, empty_bank):
@@ -172,21 +172,27 @@ def tile_attend_hop_pick_kernel(tc, xT, w1, w2, offs, offs2, out):
             cols = slice(STARTS[k], STARTS[k + 1])
             queue.dma_start(out[:, cols], result[:, cols])
 
-        first = gather_part(0)
-        second = gather_part(1)
-        finish_part(0, first, "e_codes0", "bank_out0", nc.scalar.copy)
+        pairs = [new_pairs(k, PARTS[k]) for k in range(2)]
+        for t in range(2):
+            for k in range(2):
+                pick(pairs[k][:, 0, :, t], t, STARTS[k], STARTS[k + 1])
+        grouped = []
+        for k in range(2):
+            pick(pairs[k][:, 1, :, 0], 2, STARTS[k], STARTS[k + 1], planes=1 + k)
+            pick(pairs[k][:, 1, :, 1], 3, STARTS[k], STARTS[k + 1])
+            grouped.append(weave(k, pairs[k]))
+        finish_part(0, grouped[0], "e_codes0", "bank_piece2", nc.scalar.copy)
         store(0, nc.sync)
 
         width = PARTS[2]
-        picked = held.tile([P, PACK, G - STARTS[2]], F32, tag=place(2), align_bytes=64)
-        third = held.tile([P, width, PACK], BF16, align_bytes=64)
+        late = new_pairs(2, G - STARTS[2])
         last = held.tile([P, PARTS[LAST], PACK], BF16, tag=place(LAST), align_bytes=64)
         for t in range(PACK):
             hi = G if t < 2 else STARTS[LAST]
-            pick(picked[:, t, : hi - STARTS[2]], t, STARTS[2], hi)
-        nc.scalar.copy(last[:, :, :2], picked[:, :2, width:].rearrange("p u c -> p c u"))
-        interleave(third[:], picked[:, :, :width])
-        finish_part(1, second, "e_codes1", "bank_out1", nc.scalar.copy)
+            pick(late[:, t // 2, : hi - STARTS[2], t % 2], t, STARTS[2], hi)
+        nc.scalar.copy(words(last[:])[:, :, 0:1], words(late[:, 0, :, :])[:, width:, :])
+        third = weave(2, late)
+        finish_part(1, grouped[1], "e_codes1", "bank_piece3", nc.scalar.copy)
         store(1, nc.sync)
 
         for t in range(2, PACK):

@@ -41,7 +41,7 @@ def tile_attend_hop_pick_kernel(tc, xT, w1, w2, offs, offs2, out):
         idx2 = held.tile([P, G // STRIPE], U16)
 
         x_plane = [held.tile([P, T], F32, name=f"x_plane{t}", align_bytes=64) for t in range(PACK)]
-        x_grouped = held.tile([P, N, PACK], BF16, align_bytes=64)
+        x_grouped = [held.tile([P, HALF_N, PACK], BF16, name=f"x_grouped{a}", align_bytes=64) for a in range(2)]
         x_codes = held.tile([P, N], U32, align_bytes=64, tag="x_codes")
         x_scales = held.tile([P, N], U8, align_bytes=64)
 
@@ -111,14 +111,18 @@ def tile_attend_hop_pick_kernel(tc, xT, w1, w2, offs, offs2, out):
         def first_product(bank, t, codes, cols):
             multiply(bank, codes, w1_scales[:, t, :], x_codes[:, cols], x_scales[:, cols])
 
-        for t in range(PACK - 1):
-            nc.vector.tensor_copy(x_grouped[:, :, t], x_plane[t][:].indirect(idx[:]))
         n_halves = [slice(a * HALF_N, (a + 1) * HALF_N) for a in range(2)]
-        for cols in n_halves:
-            entries = idx[:, cols.start // STRIPE : cols.stop // STRIPE]
-            nc.vector.tensor_copy(x_grouped[:, cols, PACK - 1], x_plane[PACK - 1][:].indirect(entries))
-        for cols in n_halves:
-            quantize(x_codes[:, cols], x_scales[:, cols], x_grouped[:, cols, :])
+        entries = [idx[:, cols.start // STRIPE : cols.stop // STRIPE] for cols in n_halves]
+        x_pairs = held.tile([P, 2, HALF_N, 2], BF16, align_bytes=64)
+        for t in range(PACK):
+            nc.vector.tensor_copy(x_pairs[:, t // 2, :, t % 2], x_plane[t][:].indirect(entries[1]))
+            nc.vector.tensor_copy(x_grouped[0][:, :, t], x_plane[t][:].indirect(entries[0]))
+        nc.scalar.copy(
+            x_grouped[1][:].rearrange("p c t -> p (c t)").bitcast(U32).rearrange("p (c u) -> p c u", u=2),
+            x_pairs[:].rearrange("p u c v -> p (u c v)").bitcast(U32).rearrange("p (u c) -> p c u", u=2),
+        )
+        for grouped, cols in zip(x_grouped, n_halves):
+            quantize(x_codes[:, cols], x_scales[:, cols], grouped[:])
         group_w1(nc.scalar.copy, slice(0, 2), 0)
         group_w1(nc.vector.tensor_copy, slice(2, PACK), 0)
         group_w1(nc.scalar.copy, slice(0, PACK), 1)

@@ -202,6 +202,5 @@ def tile_attend_hop_pick_kernel(tc, xT, w1, w2, offs, offs2, out):
         for t in range(2, PACK):
             pick(last[:, :, t], t, STARTS[LAST], G)
         finish_part(2, third, "e_codes2", "bank_piece0", nc.scalar.copy)
-        store(2, nc.scalar)
         finish_part(LAST, last, place(2), "bank_piece1", nc.vector.tensor_copy)
-        store(LAST, nc.sync)
+        nc.sync.dma_start(out[:, STARTS[2] :], result[:, STARTS[2] :])

@@ -18,7 +18,7 @@ LINE = 4
 HALF_N = N // 2
 PARTS = (384, 384, 192, 64)
 STARTS = tuple(sum(PARTS[:k]) for k in range(len(PARTS) + 1))
-LAST = len(PARTS) - 1
+LATE, LAST = 2, 3
 WIDTHS = (256, 128, 64)
 
 
@@ -29,6 +29,15 @@ def cut(n):
             pieces.append(slice(lo, lo + width))
             lo += width
     return pieces
+
+
+def words(grouped):
+    flat = grouped.rearrange("p c t -> p (c t)").bitcast(U32)
+    return flat.rearrange("p (c u) -> p c u", u=grouped.shape[2] // 2)
+
+
+def by_column(pairs):
+    return pairs.rearrange("p u c v -> p (u c v)").bitcast(U32).rearrange("p (u c) -> p c u", u=2)
 
 
 def tile_attend_hop_pick_kernel(tc, xT, w1, w2, offs, offs2, out):
@@ -42,7 +51,7 @@ def tile_attend_hop_pick_kernel(tc, xT, w1, w2, offs, offs2, out):
 
         x_plane = [held.tile([P, T], F32, name=f"x_plane{t}", align_bytes=64) for t in range(PACK)]
         x_grouped = [held.tile([P, HALF_N, PACK], BF16, name=f"x_grouped{a}", align_bytes=64) for a in range(2)]
-        x_codes = held.tile([P, N], U32, align_bytes=64, tag="x_codes")
+        x_codes = held.tile([P, N], U32, align_bytes=64)
         x_scales = held.tile([P, N], U8, align_bytes=64)
 
         w1_raw = held.tile([P, PACK, H], F32, align_bytes=64)
@@ -86,21 +95,15 @@ def tile_attend_hop_pick_kernel(tc, xT, w1, w2, offs, offs2, out):
                 stop=True,
             )
 
-        def interleave(grouped, planes):
-            nc.vector.tensor_copy(
-                grouped.rearrange("p (c i) t -> p c t i", i=LINE),
-                planes.rearrange("p t (c i) -> p c t i", i=LINE),
-            )
-
         def group_w1(copy, rows, q):
             copy(
                 w1_grouped[q][:, :, :, rows].rearrange("p v m j -> p m j v"),
                 w1_raw[:, rows, :].rearrange("p j (m t) -> p m j t", t=PACK)[:, :, :, 2 * q : 2 * q + 2],
             )
 
-        def quantize_w1(t0, t1, tag):
+        def quantize_w1(t0, t1):
             q = t0 // 2
-            codes = held.tile([P, t1 - t0, P], U32, name=f"w1_codes{t0}", tag=tag, align_bytes=64)
+            codes = held.tile([P, t1 - t0, P], U32, name=f"w1_codes{t0}", align_bytes=64)
             quantize(
                 codes[:].rearrange("p t m -> p (t m)"),
                 w1_scales[:, t0:t1, :].rearrange("p t m -> p (t m)"),
@@ -117,26 +120,27 @@ def tile_attend_hop_pick_kernel(tc, xT, w1, w2, offs, offs2, out):
         for t in range(PACK):
             nc.vector.tensor_copy(x_pairs[:, t // 2, :, t % 2], x_plane[t][:].indirect(entries[1]))
             nc.vector.tensor_copy(x_grouped[0][:, :, t], x_plane[t][:].indirect(entries[0]))
-        nc.scalar.copy(
-            x_grouped[1][:].rearrange("p c t -> p (c t)").bitcast(U32).rearrange("p (c u) -> p c u", u=2),
-            x_pairs[:].rearrange("p u c v -> p (u c v)").bitcast(U32).rearrange("p (u c) -> p c u", u=2),
-        )
+        nc.scalar.copy(words(x_grouped[1][:]), by_column(x_pairs[:]))
         for grouped, cols in zip(x_grouped, n_halves):
             quantize(x_codes[:, cols], x_scales[:, cols], grouped[:])
+
         group_w1(nc.scalar.copy, slice(0, 2), 0)
         group_w1(nc.vector.tensor_copy, slice(2, PACK), 0)
         group_w1(nc.scalar.copy, slice(0, PACK), 1)
 
-        codes = quantize_w1(0, 1, "w1_codes0")
+        codes = quantize_w1(0, 1)
         for a in range(PACK):
             cols = slice(a * P, (a + 1) * P)
             bank = psum.tile([P, P], F32, name=f"bank_piece{a}", tag=f"bank_piece{a}")
             first_product(bank[:], 0, codes[0], cols)
             nc.scalar.activation(h_plane[0][:, cols], bank[:], RELU)
-        codes.extend(quantize_w1(1, 2, "w1_codes1"))
+        codes.extend(quantize_w1(1, 2))
         w2_grouped = held.tile([P, M, PACK], BF16, align_bytes=64)
-        interleave(w2_grouped[:], w2_raw[:])
-        codes.extend(quantize_w1(2, PACK, "w1_codes2"))
+        nc.vector.tensor_copy(
+            w2_grouped[:].rearrange("p (c i) j -> p c j i", i=LINE),
+            w2_raw[:].rearrange("p j (c i) -> p c j i", i=LINE),
+        )
+        codes.extend(quantize_w1(2, PACK))
         quantize(w2_codes[:], w2_scales[:], w2_grouped[:])
         for t in range(1, PACK):
             bank = psum.tile([P, N], F32, name=f"bank{t}", tag=f"bank{t}")
@@ -144,63 +148,60 @@ def tile_attend_hop_pick_kernel(tc, xT, w1, w2, offs, offs2, out):
             nc.scalar.activation(h_plane[t], bank[:], RELU)
 
         def pick(dst, t, lo, hi, planes=1):
-            nc.vector.tensor_copy(dst, h_all[:, t * N : (t + planes) * N].indirect(idx2[:, lo // STRIPE : hi // STRIPE]))
+            window = h_all[:, t * N : (t + planes) * N]
+            nc.vector.tensor_copy(dst, window.indirect(idx2[:, lo // STRIPE : hi // STRIPE]))
 
-        def words(tile):
-            per_column = tile.shape[2] // 2
-            flat = tile.rearrange("p c t -> p (c t)").bitcast(U32)
-            return flat.rearrange("p (c u) -> p c u", u=per_column)
-
-        def place(k):
+        def buffer(k):
             return f"paired{k % 2}"
 
         def new_pairs(k, width):
-            return held.tile([P, 2, width, 2], BF16, name=f"e_pairs{k}", tag=place(k), align_bytes=64)
+            return held.tile([P, 2, width, 2], BF16, name=f"e_pairs{k}", tag=buffer(k), align_bytes=64)
 
         def weave(k, pairs):
-            grouped = held.tile([P, PARTS[k], PACK], BF16, name=f"e_grouped{k}", align_bytes=64)
-            both = pairs[:].rearrange("p u c v -> p (u c v)").bitcast(U32).rearrange("p (u c) -> p c u", u=2)
-            nc.scalar.copy(words(grouped[:]), both[:, : PARTS[k], :])
-            return grouped
-
-        def finish_part(k, grouped, tag, bank_tag, empty_bank):
-            e_codes = held.tile([P, PARTS[k]], U32, name=f"e_codes{k}", tag=tag, align_bytes=64)
-            e_scales = held.tile([P, PARTS[k]], U8, name=f"e_scales{k}", align_bytes=64)
-            bank = psum.tile([P, PARTS[k]], F32, name=f"bank_out{k}", tag=bank_tag)
+            pieces = []
             for cols in cut(PARTS[k]):
-                quantize(e_codes[:, cols], e_scales[:, cols], grouped[:, cols, :])
-                multiply(bank[:, cols], w2_codes[:], w2_scales[:], e_codes[:, cols], e_scales[:, cols])
-            empty_bank(result[:, STARTS[k] : STARTS[k + 1]], bank[:])
+                shape = [P, cols.stop - cols.start, PACK]
+                piece = held.tile(shape, BF16, name=f"e_grouped{k}_{cols.start}", align_bytes=64)
+                nc.scalar.copy(words(piece[:]), by_column(pairs[:])[:, cols, :])
+                pieces.append(piece)
+            return pieces
 
-        def store(k, queue):
-            cols = slice(STARTS[k], STARTS[k + 1])
-            queue.dma_start(out[:, cols], result[:, cols])
+        def finish_part(k, pieces, codes_tag, bank_tags, empty_bank):
+            e_codes = held.tile([P, PARTS[k]], U32, name=f"e_codes{k}", tag=codes_tag, align_bytes=64)
+            e_scales = held.tile([P, PARTS[k]], U8, name=f"e_scales{k}", align_bytes=64)
+            for cols, piece, bank_tag in zip(cut(PARTS[k]), pieces, bank_tags):
+                bank = psum.tile([P, cols.stop - cols.start], F32, name=f"out_{bank_tag}", tag=bank_tag)
+                quantize(e_codes[:, cols], e_scales[:, cols], piece[:])
+                multiply(bank[:], w2_codes[:], w2_scales[:], e_codes[:, cols], e_scales[:, cols])
+                empty_bank(result[:, STARTS[k] + cols.start : STARTS[k] + cols.stop], bank[:])
 
-        pairs = [new_pairs(k, PARTS[k]) for k in range(2)]
+        def store(lo, hi):
+            nc.sync.dma_start(out[:, lo:hi], result[:, lo:hi])
+
+        pairs = [new_pairs(k, PARTS[k]) for k in range(LATE)]
         for t in range(2):
-            for k in range(2):
+            for k in range(LATE):
                 pick(pairs[k][:, 0, :, t], t, STARTS[k], STARTS[k + 1])
-        grouped = []
-        for k in range(2):
+        woven = []
+        for k in range(LATE):
             pick(pairs[k][:, 1, :, 0], 2, STARTS[k], STARTS[k + 1], planes=1 + k)
             pick(pairs[k][:, 1, :, 1], 3, STARTS[k], STARTS[k + 1])
-            grouped.append(weave(k, pairs[k]))
-        finish_part(0, grouped[0], "e_codes0", "bank_piece2", nc.scalar.copy)
-        store(0, nc.sync)
+            woven.append(weave(k, pairs[k]))
+        finish_part(0, woven[0], "e_codes0", ("bank_piece2", "bank_piece3"), nc.scalar.copy)
+        store(STARTS[0], STARTS[1])
 
-        width = PARTS[2]
-        late = new_pairs(2, G - STARTS[2])
-        last = held.tile([P, PARTS[LAST], PACK], BF16, tag=place(LAST), align_bytes=64)
+        late_pairs = new_pairs(LATE, G - STARTS[LATE])
+        last_grouped = held.tile([P, PARTS[LAST], PACK], BF16, tag=buffer(LAST), align_bytes=64)
         for t in range(PACK):
             hi = G if t < 2 else STARTS[LAST]
-            pick(late[:, t // 2, : hi - STARTS[2], t % 2], t, STARTS[2], hi)
-        nc.scalar.copy(words(last[:])[:, :, 0:1], words(late[:, 0, :, :])[:, width:, :])
-        third = weave(2, late)
-        finish_part(1, grouped[1], "e_codes1", "bank_piece3", nc.scalar.copy)
-        store(1, nc.sync)
+            pick(late_pairs[:, t // 2, : hi - STARTS[LATE], t % 2], t, STARTS[LATE], hi)
+        nc.scalar.copy(words(last_grouped[:])[:, :, 0:1], words(late_pairs[:, 0, :, :])[:, PARTS[LATE] :, :])
+        late_woven = weave(LATE, late_pairs)
+        finish_part(1, woven[1], "e_codes1", ("bank2", "bank3"), nc.scalar.copy)
+        store(STARTS[1], STARTS[LATE])
 
         for t in range(2, PACK):
-            pick(last[:, :, t], t, STARTS[LAST], G)
-        finish_part(2, third, "e_codes2", "bank_piece0", nc.scalar.copy)
-        finish_part(LAST, last, place(2), "bank_piece1", nc.vector.tensor_copy)
-        nc.sync.dma_start(out[:, STARTS[2] :], result[:, STARTS[2] :])
+            pick(last_grouped[:, :, t], t, STARTS[LAST], G)
+        finish_part(LATE, late_woven, "e_codes2", ("bank_piece0", "bank1"), nc.scalar.copy)
+        finish_part(LAST, [last_grouped], buffer(LATE), ("bank_piece1",), nc.vector.tensor_copy)
+        store(STARTS[LATE], G)

@@ -5,39 +5,43 @@ FLOPS = 2 * D * H * N + 2 * H * M * G
 
 F32 = mybir.dt.float32
 BF16 = mybir.dt.bfloat16
+I32 = mybir.dt.int32
 U32 = mybir.dt.uint32
 U16 = mybir.dt.uint16
 U8 = mybir.dt.uint8
 FP8X4 = mybir.dt.float8_e4m3fn_x4
 RELU = mybir.ActivationFunctionType.Relu
+COPY = mybir.ActivationFunctionType.Copy
 
 P = 128
 PACK = 4
 STRIPE = 16
 LINE = 4
 HALF_N = N // 2
-PARTS = (384, 384, 192, 64)
-STARTS = tuple(sum(PARTS[:k]) for k in range(len(PARTS) + 1))
-LATE, LAST = 2, 3
 WIDTHS = (256, 128, 64)
+A1, A2, B1, B2, LAST = slice(0, 256), slice(256, 448), slice(448, 704), slice(704, 960), slice(960, 1024)
+
+
+def width(cols):
+    return cols.stop - cols.start
 
 
 def cut(n):
     pieces, lo = [], 0
-    for width in WIDTHS:
-        while n - lo >= width:
-            pieces.append(slice(lo, lo + width))
-            lo += width
+    for w in WIDTHS:
+        while n - lo >= w:
+            pieces.append(slice(lo, lo + w))
+            lo += w
     return pieces
 
 
-def words(grouped):
-    flat = grouped.rearrange("p c t -> p (c t)").bitcast(U32)
+def words(grouped, dtype):
+    flat = grouped.rearrange("p c t -> p (c t)").bitcast(dtype)
     return flat.rearrange("p (c u) -> p c u", u=grouped.shape[2] // 2)
 
 
-def by_column(pairs):
-    return pairs.rearrange("p u c v -> p (u c v)").bitcast(U32).rearrange("p (u c) -> p c u", u=2)
+def by_column(pairs, dtype):
+    return pairs.rearrange("p u c v -> p (u c v)").bitcast(dtype).rearrange("p (u c) -> p c u", u=2)
 
 
 def tile_attend_hop_pick_kernel(tc, xT, w1, w2, offs, offs2, out):
@@ -48,22 +52,17 @@ def tile_attend_hop_pick_kernel(tc, xT, w1, w2, offs, offs2, out):
     ):
         idx = held.tile([P, N // STRIPE], U16)
         idx2 = held.tile([P, G // STRIPE], U16)
-
         x_plane = [held.tile([P, T], F32, name=f"x_plane{t}", align_bytes=64) for t in range(PACK)]
         x_grouped = [held.tile([P, HALF_N, PACK], BF16, name=f"x_grouped{a}", align_bytes=64) for a in range(2)]
         x_codes = held.tile([P, N], U32, align_bytes=64)
         x_scales = held.tile([P, N], U8, align_bytes=64)
-
         w1_raw = held.tile([P, PACK, H], F32, align_bytes=64)
         w1_grouped = [held.tile([P, 2, P, PACK], BF16, name=f"w1_grouped{q}", align_bytes=64) for q in range(2)]
         w1_scales = held.tile([P, PACK, P], U8, align_bytes=64)
-
         w2_raw = held.tile([P, PACK, M], F32, align_bytes=64)
         w2_codes = held.tile([P, M], U32, align_bytes=64)
         w2_scales = held.tile([P, M], U8, align_bytes=64)
-
-        h_all = held.tile([P, PACK * N], F32, align_bytes=64)
-        h_plane = [h_all[:, t * N : (t + 1) * N] for t in range(PACK)]
+        h_plane = [held.tile([P, N], F32, name=f"h_plane{t}", align_bytes=64) for t in range(PACK)]
         result = held.tile([P, G], F32, align_bytes=64)
 
         x_rows = xT.rearrange("(p t) n -> p t n", t=PACK)
@@ -120,7 +119,7 @@ def tile_attend_hop_pick_kernel(tc, xT, w1, w2, offs, offs2, out):
         for t in range(PACK):
             nc.vector.tensor_copy(x_pairs[:, t // 2, :, t % 2], x_plane[t][:].indirect(entries[1]))
             nc.vector.tensor_copy(x_grouped[0][:, :, t], x_plane[t][:].indirect(entries[0]))
-        nc.scalar.copy(words(x_grouped[1][:]), by_column(x_pairs[:]))
+        nc.scalar.copy(words(x_grouped[1][:], U32), by_column(x_pairs[:], U32))
         for grouped, cols in zip(x_grouped, n_halves):
             quantize(x_codes[:, cols], x_scales[:, cols], grouped[:])
 
@@ -145,63 +144,81 @@ def tile_attend_hop_pick_kernel(tc, xT, w1, w2, offs, offs2, out):
         for t in range(1, PACK):
             bank = psum.tile([P, N], F32, name=f"bank{t}", tag=f"bank{t}")
             first_product(bank[:], t, codes[t], slice(0, N))
-            nc.scalar.activation(h_plane[t], bank[:], RELU)
+            nc.scalar.activation(h_plane[t][:], bank[:], RELU)
 
-        def pick(dst, t, lo, hi, planes=1):
-            window = h_all[:, t * N : (t + planes) * N]
-            nc.vector.tensor_copy(dst, window.indirect(idx2[:, lo // STRIPE : hi // STRIPE]))
+        def looked_up(t, cols):
+            return h_plane[t][:].indirect(idx2[:, cols.start // STRIPE : cols.stop // STRIPE])
 
-        def buffer(k):
-            return f"paired{k % 2}"
+        def grouped_tile(cols):
+            return held.tile([P, width(cols), PACK], BF16, name=f"e_grouped{cols.start}", align_bytes=64)
 
-        def new_pairs(k, width):
-            return held.tile([P, 2, width, 2], BF16, name=f"e_pairs{k}", tag=buffer(k), align_bytes=64)
+        def pairs_tile(cols):
+            return held.tile([P, 2, width(cols), 2], BF16, name=f"e_pairs{cols.start}", align_bytes=64)
 
-        def weave(k, pairs):
-            pieces = []
-            for cols in cut(PARTS[k]):
-                shape = [P, cols.stop - cols.start, PACK]
-                piece = held.tile(shape, BF16, name=f"e_grouped{k}_{cols.start}", align_bytes=64)
-                nc.scalar.copy(words(piece[:]), by_column(pairs[:])[:, cols, :])
-                pieces.append(piece)
-            return pieces
+        def pick_pair(pairs, t, cols):
+            nc.vector.tensor_copy(pairs[:, t // 2, :, t % 2], looked_up(t, cols))
 
-        def finish_part(k, pieces, codes_tag, bank_tags, empty_bank):
-            e_codes = held.tile([P, PARTS[k]], U32, name=f"e_codes{k}", tag=codes_tag, align_bytes=64)
-            e_scales = held.tile([P, PARTS[k]], U8, name=f"e_scales{k}", align_bytes=64)
-            for cols, piece, bank_tag in zip(cut(PARTS[k]), pieces, bank_tags):
-                bank = psum.tile([P, cols.stop - cols.start], F32, name=f"out_{bank_tag}", tag=bank_tag)
-                quantize(e_codes[:, cols], e_scales[:, cols], piece[:])
-                multiply(bank[:], w2_codes[:], w2_scales[:], e_codes[:, cols], e_scales[:, cols])
-                empty_bank(result[:, STARTS[k] + cols.start : STARTS[k] + cols.stop], bank[:])
+        def weave(pairs, cols):
+            grouped = grouped_tile(cols)
+            nc.vector.tensor_copy(words(grouped[:], I32), by_column(pairs[:], I32))
+            return grouped
+
+        def pick_planes(cols):
+            planes = held.tile([P, PACK, width(cols)], BF16, name=f"e_planes{cols.start}", align_bytes=64)
+            for t in range(PACK):
+                nc.scalar.activation(planes[:, t, :], looked_up(t, cols), COPY)
+            return planes
+
+        def interleave(planes, cols):
+            grouped = grouped_tile(cols)
+            nc.vector.tensor_copy(
+                grouped[:].rearrange("p (c i) t -> p c t i", i=LINE),
+                planes[:].rearrange("p t (c i) -> p c t i", i=LINE),
+            )
+            return grouped
+
+        def product(cols, grouped, bank_tags):
+            e_codes = held.tile([P, width(cols)], U32, name=f"e_codes{cols.start}", align_bytes=64)
+            e_scales = held.tile([P, width(cols)], U8, name=f"e_scales{cols.start}", align_bytes=64)
+            banks = []
+            for piece, bank_tag in zip(cut(width(cols)), bank_tags):
+                bank = psum.tile([P, width(piece)], F32, name=f"out_{bank_tag}", tag=bank_tag)
+                quantize(e_codes[:, piece], e_scales[:, piece], grouped[:, piece, :])
+                multiply(bank[:], w2_codes[:], w2_scales[:], e_codes[:, piece], e_scales[:, piece])
+                banks.append((slice(cols.start + piece.start, cols.start + piece.stop), bank))
+            return banks
+
+        def empty(copy, banks):
+            for cols, bank in banks:
+                copy(result[:, cols], bank[:])
 
         def store(lo, hi):
             nc.sync.dma_start(out[:, lo:hi], result[:, lo:hi])
 
-        pairs = [new_pairs(k, PARTS[k]) for k in range(LATE)]
+        planes1 = pick_planes(B1)
+        planes2 = pick_planes(B2)
+        pairs1, pairs2 = pairs_tile(A1), pairs_tile(A2)
         for t in range(2):
-            for k in range(LATE):
-                pick(pairs[k][:, 0, :, t], t, STARTS[k], STARTS[k + 1])
-        woven = []
-        for k in range(LATE):
-            pick(pairs[k][:, 1, :, 0], 2, STARTS[k], STARTS[k + 1], planes=1 + k)
-            pick(pairs[k][:, 1, :, 1], 3, STARTS[k], STARTS[k + 1])
-            woven.append(weave(k, pairs[k]))
-        finish_part(0, woven[0], "e_codes0", ("bank_piece2", "bank_piece3"), nc.scalar.copy)
-        store(STARTS[0], STARTS[1])
-
-        late_pairs = new_pairs(LATE, G - STARTS[LATE])
-        last_grouped = held.tile([P, PARTS[LAST], PACK], BF16, tag=buffer(LAST), align_bytes=64)
-        for t in range(PACK):
-            hi = G if t < 2 else STARTS[LAST]
-            pick(late_pairs[:, t // 2, : hi - STARTS[LATE], t % 2], t, STARTS[LATE], hi)
-        nc.scalar.copy(words(last_grouped[:])[:, :, 0:1], words(late_pairs[:, 0, :, :])[:, PARTS[LATE] :, :])
-        late_woven = weave(LATE, late_pairs)
-        finish_part(1, woven[1], "e_codes1", ("bank2", "bank3"), nc.scalar.copy)
-        store(STARTS[1], STARTS[LATE])
-
+            pick_pair(pairs1, t, A1)
+            pick_pair(pairs2, t, A2)
+        pick_pair(pairs1, 2, A1)
+        pick_pair(pairs1, 3, A1)
+        pick_pair(pairs2, 2, A2)
+        woven1 = weave(pairs1, A1)
+        pick_pair(pairs2, 3, A2)
+        banks = product(A1, woven1, ("bank_piece0",))
+        woven2 = weave(pairs2, A2)
+        inter1 = interleave(planes1, B1)
+        banks.extend(product(A2, woven2, ("bank_piece1", "bank_piece2")))
+        last_grouped = grouped_tile(LAST)
+        nc.vector.tensor_copy(last_grouped[:, :, 0], looked_up(0, LAST))
+        banks.extend(product(B1, inter1, ("bank_piece3",)))
+        empty(nc.scalar.copy, banks)
+        store(A1.start, B1.stop)
+        nc.vector.tensor_copy(last_grouped[:, :, 1], looked_up(1, LAST))
+        inter2 = interleave(planes2, B2)
         for t in range(2, PACK):
-            pick(last_grouped[:, :, t], t, STARTS[LAST], G)
-        finish_part(LATE, late_woven, "e_codes2", ("bank_piece0", "bank1"), nc.scalar.copy)
-        finish_part(LAST, [last_grouped], buffer(LATE), ("bank_piece1",), nc.vector.tensor_copy)
-        store(STARTS[LATE], G)
+            nc.vector.tensor_copy(last_grouped[:, :, t], looked_up(t, LAST))
+        empty(nc.scalar.copy, product(B2, inter2, ("bank1",)))
+        empty(nc.vector.tensor_copy, product(LAST, last_grouped, ("bank2",)))
+        store(B2.start, G)

@@ -19,7 +19,7 @@ STRIPE = 16
 LINE = 4
 HALF_N = N // 2
 WIDTHS = (256, 128, 64)
-A1, A2, B1, B2, LAST = slice(0, 256), slice(256, 448), slice(448, 704), slice(704, 960), slice(960, 1024)
+A1, A2, B1, B2, B3 = slice(0, 256), slice(256, 448), slice(448, 704), slice(704, 896), slice(896, 1024)
 
 
 def width(cols):
@@ -169,24 +169,35 @@ def tile_attend_hop_pick_kernel(tc, xT, w1, w2, offs, offs2, out):
                 nc.scalar.activation(planes[:, t, :], looked_up(t, cols), COPY)
             return planes
 
-        def interleave(planes, cols):
-            grouped = grouped_tile(cols)
-            nc.vector.tensor_copy(
-                grouped[:].rearrange("p (c i) t -> p c t i", i=LINE),
-                planes[:].rearrange("p t (c i) -> p c t i", i=LINE),
-            )
-            return grouped
+        def interleave(planes, cols, widths):
+            pieces, lo = [], 0
+            for w in widths:
+                piece = slice(cols.start + lo, cols.start + lo + w)
+                grouped = grouped_tile(piece)
+                nc.vector.tensor_copy(
+                    grouped[:].rearrange("p (c i) t -> p c t i", i=LINE),
+                    planes[:, :, lo : lo + w].rearrange("p t (c i) -> p c t i", i=LINE),
+                )
+                pieces.append((piece, grouped[:]))
+                lo += w
+            return pieces
 
-        def product(cols, grouped, bank_tags):
-            e_codes = held.tile([P, width(cols)], U32, name=f"e_codes{cols.start}", align_bytes=64)
-            e_scales = held.tile([P, width(cols)], U8, name=f"e_scales{cols.start}", align_bytes=64)
+        def product(pieces, bank_tags):
             banks = []
-            for piece, bank_tag in zip(cut(width(cols)), bank_tags):
-                bank = psum.tile([P, width(piece)], F32, name=f"out_{bank_tag}", tag=bank_tag)
-                quantize(e_codes[:, piece], e_scales[:, piece], grouped[:, piece, :])
-                multiply(bank[:], w2_codes[:], w2_scales[:], e_codes[:, piece], e_scales[:, piece])
-                banks.append((slice(cols.start + piece.start, cols.start + piece.stop), bank))
+            for (cols, grouped), bank_tag in zip(pieces, bank_tags):
+                e_codes = held.tile([P, width(cols)], U32, name=f"e_codes{cols.start}", align_bytes=64)
+                e_scales = held.tile([P, width(cols)], U8, name=f"e_scales{cols.start}", align_bytes=64)
+                bank = psum.tile([P, width(cols)], F32, name=f"out_{bank_tag}", tag=bank_tag)
+                quantize(e_codes[:], e_scales[:], grouped)
+                multiply(bank[:], w2_codes[:], w2_scales[:], e_codes[:], e_scales[:])
+                banks.append((cols, bank))
             return banks
+
+        def pieces_of(cols, grouped):
+            return [
+                (slice(cols.start + piece.start, cols.start + piece.stop), grouped[:, piece, :])
+                for piece in cut(width(cols))
+            ]
 
         def empty(copy, banks):
             for cols, bank in banks:
@@ -195,30 +206,22 @@ def tile_attend_hop_pick_kernel(tc, xT, w1, w2, offs, offs2, out):
         def store(lo, hi):
             nc.sync.dma_start(out[:, lo:hi], result[:, lo:hi])
 
-        planes1 = pick_planes(B1)
-        planes2 = pick_planes(B2)
+        planes = [pick_planes(cols) for cols in (B1, B2, B3)]
         pairs1, pairs2 = pairs_tile(A1), pairs_tile(A2)
-        for t in range(2):
+        for t in range(PACK):
             pick_pair(pairs1, t, A1)
             pick_pair(pairs2, t, A2)
-        pick_pair(pairs1, 2, A1)
-        pick_pair(pairs1, 3, A1)
-        pick_pair(pairs2, 2, A2)
         woven1 = weave(pairs1, A1)
-        pick_pair(pairs2, 3, A2)
-        banks = product(A1, woven1, ("bank_piece0",))
         woven2 = weave(pairs2, A2)
-        inter1 = interleave(planes1, B1)
-        banks.extend(product(A2, woven2, ("bank_piece1", "bank_piece2")))
-        last_grouped = grouped_tile(LAST)
-        nc.vector.tensor_copy(last_grouped[:, :, 0], looked_up(0, LAST))
-        banks.extend(product(B1, inter1, ("bank_piece3",)))
+        empty(nc.vector.tensor_copy, product(pieces_of(A1, woven1), ("bank_piece0",)))
+        store(A1.start, A1.stop)
+        banks = product(pieces_of(A2, woven2), ("bank_piece1", "bank_piece2"))
+        banks.extend(product(interleave(planes[0], B1, (128, 128)), ("bank_piece3", "bank1")))
         empty(nc.scalar.copy, banks)
-        store(A1.start, B1.stop)
-        nc.vector.tensor_copy(last_grouped[:, :, 1], looked_up(1, LAST))
-        inter2 = interleave(planes2, B2)
-        for t in range(2, PACK):
-            nc.vector.tensor_copy(last_grouped[:, :, t], looked_up(t, LAST))
-        empty(nc.scalar.copy, product(B2, inter2, ("bank1",)))
-        empty(nc.vector.tensor_copy, product(LAST, last_grouped, ("bank2",)))
-        store(B2.start, G)
+        store(A2.start, B1.stop)
+        empty(nc.scalar.copy, product(interleave(planes[1], B2, (128, 64)), ("bank2", "bank3")))
+        store(B2.start, B2.stop)
+        banks = product(interleave(planes[2], B3, (64, 64)), ("bank_piece0", "bank_spare"))
+        empty(nc.scalar.copy, banks[:1])
+        empty(nc.vector.tensor_copy, banks[1:])
+        store(B3.start, G)

@@ -19,7 +19,7 @@ STRIPE = 16
 LINE = 4
 HALF_N = N // 2
 WIDTHS = (256, 128, 64)
-A1, A2, B1, B2, B3 = slice(0, 256), slice(256, 448), slice(448, 704), slice(704, 896), slice(896, 1024)
+A1, A2, B1, B2, B3 = slice(0, 256), slice(256, 512), slice(512, 768), slice(768, 896), slice(896, 1024)
 
 
 def width(cols):
@@ -54,11 +54,11 @@ def tile_attend_hop_pick_kernel(tc, xT, w1, w2, offs, offs2, out):
         idx2 = held.tile([P, G // STRIPE], U16)
         x_plane = [held.tile([P, T], F32, name=f"x_plane{t}", align_bytes=64) for t in range(PACK)]
         x_grouped = [held.tile([P, HALF_N, PACK], BF16, name=f"x_grouped{a}", align_bytes=64) for a in range(2)]
-        x_codes = held.tile([P, N], U32, align_bytes=64)
-        x_scales = held.tile([P, N], U8, align_bytes=64)
+        x_codes = held.tile([P, N], U32, tag="x_codes", align_bytes=64)
+        x_scales = held.tile([P, N], U8, tag="x_scales", align_bytes=64)
         w1_raw = held.tile([P, PACK, H], F32, align_bytes=64)
         w1_grouped = [held.tile([P, 2, P, PACK], BF16, name=f"w1_grouped{q}", align_bytes=64) for q in range(2)]
-        w1_scales = held.tile([P, PACK, P], U8, align_bytes=64)
+        w1_scales = held.tile([P, PACK, P], U8, tag="w1_scales", align_bytes=64)
         w2_raw = held.tile([P, PACK, M], F32, align_bytes=64)
         w2_codes = held.tile([P, M], U32, align_bytes=64)
         w2_scales = held.tile([P, M], U8, align_bytes=64)
@@ -163,8 +163,8 @@ def tile_attend_hop_pick_kernel(tc, xT, w1, w2, offs, offs2, out):
             nc.vector.tensor_copy(words(grouped[:], I32), by_column(pairs[:], I32))
             return grouped
 
-        def pick_planes(cols):
-            planes = held.tile([P, PACK, width(cols)], BF16, name=f"e_planes{cols.start}", align_bytes=64)
+        def pick_planes(cols, tag):
+            planes = held.tile([P, PACK, width(cols)], BF16, name=f"e_planes{cols.start}", tag=tag, align_bytes=64)
             for t in range(PACK):
                 nc.scalar.activation(planes[:, t, :], looked_up(t, cols), COPY)
             return planes
@@ -206,7 +206,7 @@ def tile_attend_hop_pick_kernel(tc, xT, w1, w2, offs, offs2, out):
         def store(lo, hi):
             nc.sync.dma_start(out[:, lo:hi], result[:, lo:hi])
 
-        planes = [pick_planes(cols) for cols in (B1, B2, B3)]
+        planes = [pick_planes(cols, tag) for cols, tag in ((B1, "x_codes"), (B2, "x_scales"), (B3, "w1_scales"))]
         pairs1, pairs2 = pairs_tile(A1), pairs_tile(A2)
         for t in range(PACK):
             pick_pair(pairs1, t, A1)
@@ -215,13 +215,13 @@ def tile_attend_hop_pick_kernel(tc, xT, w1, w2, offs, offs2, out):
         woven2 = weave(pairs2, A2)
         empty(nc.vector.tensor_copy, product(pieces_of(A1, woven1), ("bank_piece0",)))
         store(A1.start, A1.stop)
-        banks = product(pieces_of(A2, woven2), ("bank_piece1", "bank_piece2"))
-        banks.extend(product(interleave(planes[0], B1, (128, 128)), ("bank_piece3", "bank1")))
+        banks = product(pieces_of(A2, woven2), ("bank_piece1",))
+        banks.extend(product(interleave(planes[0], B1, (128, 128)), ("bank_piece2", "bank_piece3")))
         empty(nc.scalar.copy, banks)
         store(A2.start, B1.stop)
-        empty(nc.scalar.copy, product(interleave(planes[1], B2, (128, 64)), ("bank2", "bank3")))
+        empty(nc.scalar.copy, product(interleave(planes[1], B2, (64, 64)), ("bank1", "bank2")))
         store(B2.start, B2.stop)
-        banks = product(interleave(planes[2], B3, (64, 64)), ("bank_piece0", "bank_spare"))
+        banks = product(interleave(planes[2], B3, (64, 64)), ("bank3", "bank_spare"))
         empty(nc.scalar.copy, banks[:1])
         empty(nc.vector.tensor_copy, banks[1:])
         store(B3.start, G)

@@ -206,22 +206,21 @@ def tile_attend_hop_pick_kernel(tc, xT, w1, w2, offs, offs2, out):
         def store(lo, hi):
             nc.sync.dma_start(out[:, lo:hi], result[:, lo:hi])
 
-        planes = [pick_planes(cols, tag) for cols, tag in ((B1, "x_codes"), (B2, "x_scales"), (B3, "w1_scales"))]
+        planes = [pick_planes(cols, tag) for cols, tag in ((B1, "x_codes"), (B2, "planes_free"), (B3, "x_scales"))]
         pairs1, pairs2 = pairs_tile(A1), pairs_tile(A2)
         for t in range(PACK):
             pick_pair(pairs1, t, A1)
             pick_pair(pairs2, t, A2)
         woven1 = weave(pairs1, A1)
         woven2 = weave(pairs2, A2)
-        empty(nc.vector.tensor_copy, product(pieces_of(A1, woven1), ("bank_piece0",)))
-        store(A1.start, A1.stop)
-        banks = product(pieces_of(A2, woven2), ("bank_piece1",))
-        banks.extend(product(interleave(planes[0], B1, (128, 128)), ("bank_piece2", "bank_piece3")))
-        empty(nc.scalar.copy, banks)
-        store(A2.start, B1.stop)
-        empty(nc.scalar.copy, product(interleave(planes[1], B2, (64, 64)), ("bank1", "bank2")))
-        store(B2.start, B2.stop)
-        banks = product(interleave(planes[2], B3, (64, 64)), ("bank3", "bank_spare"))
-        empty(nc.scalar.copy, banks[:1])
-        empty(nc.vector.tensor_copy, banks[1:])
+        own = product(pieces_of(A1, woven1) + pieces_of(A2, woven2), ("bank_piece0", "bank_piece1"))
+        pieces = interleave(planes[0], B1, (256,)) + interleave(planes[1], B2, (128,))
+        middle = product(pieces, ("bank_piece2", "bank_piece3"))
+        late = product(interleave(planes[2], B3, (64, 64)), ("bank1", "bank2"))
+        empty(nc.scalar.copy, own)
+        store(A1.start, A2.stop)
+        empty(nc.scalar.copy, middle)
+        store(B1.start, B2.stop)
+        empty(nc.scalar.copy, late[:1])
+        empty(nc.vector.tensor_copy, late[1:])
         store(B3.start, G)

@@ -116,15 +116,21 @@ def tile_attend_hop_pick_kernel(tc, xT, w1, w2, offs, offs2, out):
         n_halves = [slice(a * HALF_N, (a + 1) * HALF_N) for a in range(2)]
         entries = [idx[:, cols.start // STRIPE : cols.stop // STRIPE] for cols in n_halves]
         x_pairs = held.tile([P, 2, HALF_N, 2], BF16, align_bytes=64)
+        x_picked = held.tile([P, PACK, HALF_N], BF16, align_bytes=64)
         for t in range(PACK):
             nc.vector.tensor_copy(x_pairs[:, t // 2, :, t % 2], x_plane[t][:].indirect(entries[1]))
-            nc.vector.tensor_copy(x_grouped[0][:, :, t], x_plane[t][:].indirect(entries[0]))
+            nc.scalar.activation(x_picked[:, t, :], x_plane[t][:].indirect(entries[0]), COPY)
+            nc.vector.tensor_copy(x_grouped[0][:, :, t], x_picked[:, t, :])
         nc.scalar.copy(words(x_grouped[1][:], U32), by_column(x_pairs[:], U32))
         for grouped, cols in zip(x_grouped, n_halves):
             quantize(x_codes[:, cols], x_scales[:, cols], grouped[:])
 
         group_w1(nc.scalar.copy, slice(0, 2), 0)
-        group_w1(nc.vector.tensor_copy, slice(2, PACK), 0)
+        for t in range(2):
+            nc.vector.tensor_copy(
+                w1_grouped[0][:, t, :, 2:PACK],
+                w1_raw[:, 2:PACK, :].rearrange("p j (m t) -> p t m j", t=PACK)[:, t, :, :],
+            )
         group_w1(nc.scalar.copy, slice(0, PACK), 1)
 
         codes = quantize_w1(0, 1)

@@ -19,7 +19,7 @@ STRIPE = 16
 LINE = 4
 HALF_N = N // 2
 WIDTHS = (256, 128, 64)
-A1, A2, B1, B2, B3 = slice(0, 256), slice(256, 512), slice(512, 768), slice(768, 896), slice(896, 1024)
+A1, A2, B1, B2, B3 = slice(0, 256), slice(256, 512), slice(512, 768), slice(768, 960), slice(960, 1024)
 
 
 def width(cols):
@@ -53,7 +53,6 @@ def tile_attend_hop_pick_kernel(tc, xT, w1, w2, offs, offs2, out):
         idx = held.tile([P, N // STRIPE], U16)
         idx2 = held.tile([P, G // STRIPE], U16)
         x_plane = [held.tile([P, T], F32, name=f"x_plane{t}", align_bytes=64) for t in range(PACK)]
-        x_grouped = [held.tile([P, HALF_N, PACK], BF16, name=f"x_grouped{a}", align_bytes=64) for a in range(2)]
         x_codes = held.tile([P, N], U32, tag="x_codes", align_bytes=64)
         x_scales = held.tile([P, N], U8, tag="x_scales", align_bytes=64)
         w1_raw = held.tile([P, PACK, H], F32, align_bytes=64)
@@ -113,17 +112,25 @@ def tile_attend_hop_pick_kernel(tc, xT, w1, w2, offs, offs2, out):
         def first_product(bank, t, codes, cols):
             multiply(bank, codes, w1_scales[:, t, :], x_codes[:, cols], x_scales[:, cols])
 
-        n_halves = [slice(a * HALF_N, (a + 1) * HALF_N) for a in range(2)]
-        entries = [idx[:, cols.start // STRIPE : cols.stop // STRIPE] for cols in n_halves]
+        def listed(t, cols):
+            return x_plane[t][:].indirect(idx[:, cols.start // STRIPE : cols.stop // STRIPE])
+
+        quarters = [slice(a * P, (a + 1) * P) for a in range(2)]
+        upper = slice(HALF_N, N)
+        x_picked = [held.tile([P, PACK, P], BF16, name=f"x_picked{a}", align_bytes=64) for a in range(2)]
+        x_placed = [held.tile([P, P, PACK], BF16, name=f"x_placed{a}", align_bytes=64) for a in range(2)]
         x_pairs = held.tile([P, 2, HALF_N, 2], BF16, align_bytes=64)
-        x_picked = held.tile([P, PACK, HALF_N], BF16, align_bytes=64)
+        x_woven = held.tile([P, HALF_N, PACK], BF16, align_bytes=64)
         for t in range(PACK):
-            nc.vector.tensor_copy(x_pairs[:, t // 2, :, t % 2], x_plane[t][:].indirect(entries[1]))
-            nc.scalar.activation(x_picked[:, t, :], x_plane[t][:].indirect(entries[0]), COPY)
-            nc.vector.tensor_copy(x_grouped[0][:, :, t], x_picked[:, t, :])
-        nc.scalar.copy(words(x_grouped[1][:], U32), by_column(x_pairs[:], U32))
-        for grouped, cols in zip(x_grouped, n_halves):
-            quantize(x_codes[:, cols], x_scales[:, cols], grouped[:])
+            nc.vector.tensor_copy(x_pairs[:, t // 2, :, t % 2], listed(t, upper))
+            for picked, placed, cols in zip(x_picked, x_placed, quarters):
+                nc.scalar.activation(picked[:, t, :], listed(t, cols), COPY)
+                nc.vector.tensor_copy(placed[:, :, t], picked[:, t, :])
+        nc.scalar.copy(words(x_woven[:], U32)[:, quarters[0], :], by_column(x_pairs[:], U32)[:, quarters[0], :])
+        nc.vector.tensor_copy(words(x_woven[:], I32)[:, quarters[1], :], by_column(x_pairs[:], I32)[:, quarters[1], :])
+        for placed, cols in zip(x_placed, quarters):
+            quantize(x_codes[:, cols], x_scales[:, cols], placed[:])
+        quantize(x_codes[:, upper], x_scales[:, upper], x_woven[:])
 
         group_w1(nc.scalar.copy, slice(0, 2), 0)
         for t in range(2):
@@ -220,13 +227,12 @@ def tile_attend_hop_pick_kernel(tc, xT, w1, w2, offs, offs2, out):
         woven1 = weave(pairs1, A1)
         woven2 = weave(pairs2, A2)
         own = product(pieces_of(A1, woven1) + pieces_of(A2, woven2), ("bank_piece0", "bank_piece1"))
-        pieces = interleave(planes[0], B1, (256,)) + interleave(planes[1], B2, (128,))
-        middle = product(pieces, ("bank_piece2", "bank_piece3"))
-        late = product(interleave(planes[2], B3, (64, 64)), ("bank1", "bank2"))
-        empty(nc.scalar.copy, own)
-        store(A1.start, A2.stop)
-        empty(nc.scalar.copy, middle)
-        store(B1.start, B2.stop)
+        pieces = interleave(planes[0], B1, (256,)) + interleave(planes[1], B2, (128, 64))
+        banks = own + product(pieces[:2], ("bank_piece2", "bank_piece3"))
+        late = product(pieces[2:] + interleave(planes[2], B3, (64,)), ("bank1", "bank2"))
+        for cols, bank in banks:
+            nc.scalar.copy(result[:, cols], bank[:])
+            store(cols.start, cols.stop)
         empty(nc.scalar.copy, late[:1])
         empty(nc.vector.tensor_copy, late[1:])
-        store(B3.start, G)
+        store(B2.start + 128, G)

@@ -19,7 +19,7 @@ STRIPE = 16
 LINE = 4
 HALF_N = N // 2
 WIDTHS = (256, 128, 64)
-A1, A2, B1, B2, B3 = slice(0, 256), slice(256, 512), slice(512, 768), slice(768, 960), slice(960, 1024)
+A1, A2, B1, B2, B3 = slice(0, 256), slice(256, 448), slice(448, 704), slice(704, 896), slice(896, 1024)
 
 
 def width(cols):
@@ -177,7 +177,7 @@ def tile_attend_hop_pick_kernel(tc, xT, w1, w2, offs, offs2, out):
             return grouped
 
         def pick_planes(cols, tag):
-            planes = held.tile([P, PACK, width(cols)], BF16, name=f"e_planes{cols.start}", tag=tag, align_bytes=64)
+            planes = held.tile([P, PACK, width(cols)], F32, name=f"e_planes{cols.start}", tag=tag, align_bytes=64)
             for t in range(PACK):
                 nc.scalar.activation(planes[:, t, :], looked_up(t, cols), COPY)
             return planes
@@ -226,13 +226,13 @@ def tile_attend_hop_pick_kernel(tc, xT, w1, w2, offs, offs2, out):
             pick_pair(pairs2, t, A2)
         woven1 = weave(pairs1, A1)
         woven2 = weave(pairs2, A2)
-        own = product(pieces_of(A1, woven1) + pieces_of(A2, woven2), ("bank_piece0", "bank_piece1"))
+        banks = product(pieces_of(A1, woven1) + pieces_of(A2, woven2), ("bank_piece0", "bank_piece1", "bank_piece2"))
         pieces = interleave(planes[0], B1, (256,)) + interleave(planes[1], B2, (128, 64))
-        banks = own + product(pieces[:2], ("bank_piece2", "bank_piece3"))
-        late = product(pieces[2:] + interleave(planes[2], B3, (64,)), ("bank1", "bank2"))
-        for cols, bank in banks:
-            nc.scalar.copy(result[:, cols], bank[:])
-            store(cols.start, cols.stop)
+        banks.extend(product(pieces, ("bank_piece3", "bank1", "bank2")))
+        late = product(interleave(planes[2], B3, (64, 64)), ("bank3", "bank_spare"))
+        for part, first, last in ((A1, 0, 1), (A2, 1, 3), (B1, 3, 4), (B2, 4, 6)):
+            empty(nc.scalar.copy, banks[first:last])
+            store(part.start, part.stop)
         empty(nc.scalar.copy, late[:1])
         empty(nc.vector.tensor_copy, late[1:])
-        store(B2.start + 128, G)
+        store(B3.start, G)

@@ -19,7 +19,7 @@ STRIPE = 16
 LINE = 4
 HALF_N = N // 2
 WIDTHS = (256, 128, 64)
-A1, A2, B1, B2, B3 = slice(0, 256), slice(256, 448), slice(448, 704), slice(704, 896), slice(896, 1024)
+A1, A2, B1, B2, B3 = slice(0, 256), slice(256, 480), slice(480, 768), slice(768, 896), slice(896, 1024)
 
 
 def width(cols):
@@ -171,10 +171,8 @@ def tile_attend_hop_pick_kernel(tc, xT, w1, w2, offs, offs2, out):
         def pick_pair(pairs, t, cols):
             nc.vector.tensor_copy(pairs[:, t // 2, :, t % 2], looked_up(t, cols))
 
-        def weave(pairs, cols):
-            grouped = grouped_tile(cols)
-            nc.vector.tensor_copy(words(grouped[:], I32), by_column(pairs[:], I32))
-            return grouped
+        def weave(grouped, pairs, lo, hi):
+            nc.vector.tensor_copy(words(grouped, I32), by_column(pairs[:], I32)[:, lo:hi, :])
 
         def pick_planes(cols, tag):
             planes = held.tile([P, PACK, width(cols)], F32, name=f"e_planes{cols.start}", tag=tag, align_bytes=64)
@@ -182,18 +180,11 @@ def tile_attend_hop_pick_kernel(tc, xT, w1, w2, offs, offs2, out):
                 nc.scalar.activation(planes[:, t, :], looked_up(t, cols), COPY)
             return planes
 
-        def interleave(planes, cols, widths):
-            pieces, lo = [], 0
-            for w in widths:
-                piece = slice(cols.start + lo, cols.start + lo + w)
-                grouped = grouped_tile(piece)
-                nc.vector.tensor_copy(
-                    grouped[:].rearrange("p (c i) t -> p c t i", i=LINE),
-                    planes[:, :, lo : lo + w].rearrange("p t (c i) -> p c t i", i=LINE),
-                )
-                pieces.append((piece, grouped[:]))
-                lo += w
-            return pieces
+        def interleave(grouped, planes):
+            nc.vector.tensor_copy(
+                grouped.rearrange("p (c i) t -> p c t i", i=LINE),
+                planes.rearrange("p t (c i) -> p c t i", i=LINE),
+            )
 
         def product(pieces, bank_tags):
             banks = []
@@ -205,12 +196,6 @@ def tile_attend_hop_pick_kernel(tc, xT, w1, w2, offs, offs2, out):
                 multiply(bank[:], w2_codes[:], w2_scales[:], e_codes[:], e_scales[:])
                 banks.append((cols, bank))
             return banks
-
-        def pieces_of(cols, grouped):
-            return [
-                (slice(cols.start + piece.start, cols.start + piece.stop), grouped[:, piece, :])
-                for piece in cut(width(cols))
-            ]
 
         def empty(copy, banks):
             for cols, bank in banks:
@@ -224,15 +209,22 @@ def tile_attend_hop_pick_kernel(tc, xT, w1, w2, offs, offs2, out):
         for t in range(PACK):
             pick_pair(pairs1, t, A1)
             pick_pair(pairs2, t, A2)
-        woven1 = weave(pairs1, A1)
-        woven2 = weave(pairs2, A2)
-        banks = product(pieces_of(A1, woven1) + pieces_of(A2, woven2), ("bank_piece0", "bank_piece1", "bank_piece2"))
-        pieces = interleave(planes[0], B1, (256,)) + interleave(planes[1], B2, (128, 64))
-        banks.extend(product(pieces, ("bank_piece3", "bank1", "bank2")))
-        late = product(interleave(planes[2], B3, (64, 64)), ("bank3", "bank_spare"))
-        for part, first, last in ((A1, 0, 1), (A2, 1, 3), (B1, 3, 4), (B2, 4, 6)):
-            empty(nc.scalar.copy, banks[first:last])
-            store(part.start, part.stop)
+        first, middle, free = grouped_tile(A1), grouped_tile(slice(A2.start, B1.stop)), grouped_tile(B2)
+        ends = [slice(B3.start, B3.start + 64), slice(B3.start + 64, G)]
+        last = [grouped_tile(cols) for cols in ends]
+        weave(first[:], pairs1, 0, width(A1))
+        weave(middle[:, 0 : width(A2), :], pairs2, 0, width(A2))
+        banks = product([(A1, first[:])], ("bank_piece0",))
+        interleave(middle[:, width(A2) : 512, :], planes[0][:])
+        interleave(free[:], planes[1][:])
+        pieces = [(slice(256, 512), middle[:, 0:256, :]), (slice(512, 768), middle[:, 256:512, :]), (B2, free[:])]
+        banks.extend(product(pieces, ("bank_piece1", "bank_piece2", "bank_piece3")))
+        for k in range(2):
+            interleave(last[k][:], planes[2][:, :, 64 * k : 64 * (k + 1)])
+        late = product([(cols, tile[:]) for cols, tile in zip(ends, last)], ("bank1", "bank2"))
+        for cols, bank in banks:
+            nc.scalar.copy(result[:, cols], bank[:])
+            store(cols.start, cols.stop)
         empty(nc.scalar.copy, late[:1])
         empty(nc.vector.tensor_copy, late[1:])
         store(B3.start, G)

@@ -12,27 +12,21 @@ U8 = mybir.dt.uint8
 FP8X4 = mybir.dt.float8_e4m3fn_x4
 RELU = mybir.ActivationFunctionType.Relu
 COPY = mybir.ActivationFunctionType.Copy
+MULT = mybir.AluOpType.mult
+ADD = mybir.AluOpType.add
 
 P = 128
 PACK = 4
 STRIPE = 16
 LINE = 4
 HALF_N = N // 2
-WIDTHS = (256, 128, 64)
-A1, A2, B1, B2, B3 = slice(0, 256), slice(256, 480), slice(480, 768), slice(768, 896), slice(896, 1024)
+A1, A2 = slice(0, 256), slice(256, 544)
+C1, C2 = slice(544, 672), slice(672, 768)
+B2, B3 = slice(768, 896), slice(896, 1024)
 
 
 def width(cols):
     return cols.stop - cols.start
-
-
-def cut(n):
-    pieces, lo = [], 0
-    for w in WIDTHS:
-        while n - lo >= w:
-            pieces.append(slice(lo, lo + w))
-            lo += w
-    return pieces
 
 
 def words(grouped, dtype):
@@ -168,14 +162,11 @@ def tile_attend_hop_pick_kernel(tc, xT, w1, w2, offs, offs2, out):
         def pairs_tile(cols):
             return held.tile([P, 2, width(cols), 2], BF16, name=f"e_pairs{cols.start}", align_bytes=64)
 
-        def pick_pair(pairs, t, cols):
-            nc.vector.tensor_copy(pairs[:, t // 2, :, t % 2], looked_up(t, cols))
+        def weave(grouped, pairs):
+            nc.vector.tensor_copy(words(grouped, I32), by_column(pairs[:], I32))
 
-        def weave(grouped, pairs, lo, hi):
-            nc.vector.tensor_copy(words(grouped, I32), by_column(pairs[:], I32)[:, lo:hi, :])
-
-        def pick_planes(cols, tag):
-            planes = held.tile([P, PACK, width(cols)], F32, name=f"e_planes{cols.start}", tag=tag, align_bytes=64)
+        def pick_planes(cols, dtype, tag):
+            planes = held.tile([P, PACK, width(cols)], dtype, name=f"e_planes{cols.start}", tag=tag, align_bytes=64)
             for t in range(PACK):
                 nc.scalar.activation(planes[:, t, :], looked_up(t, cols), COPY)
             return planes
@@ -186,45 +177,44 @@ def tile_attend_hop_pick_kernel(tc, xT, w1, w2, offs, offs2, out):
                 planes.rearrange("p t (c i) -> p c t i", i=LINE),
             )
 
-        def product(pieces, bank_tags):
-            banks = []
-            for (cols, grouped), bank_tag in zip(pieces, bank_tags):
-                e_codes = held.tile([P, width(cols)], U32, name=f"e_codes{cols.start}", align_bytes=64)
-                e_scales = held.tile([P, width(cols)], U8, name=f"e_scales{cols.start}", align_bytes=64)
-                bank = psum.tile([P, width(cols)], F32, name=f"out_{bank_tag}", tag=bank_tag)
-                quantize(e_codes[:], e_scales[:], grouped)
-                multiply(bank[:], w2_codes[:], w2_scales[:], e_codes[:], e_scales[:])
-                banks.append((cols, bank))
-            return banks
+        def interleave_aside(grouped, planes):
+            nc.gpsimd.tensor_scalar(grouped, planes.rearrange("p t c -> p c t"), 1.0, 0.0, MULT, ADD)
 
-        def empty(copy, banks):
-            for cols, bank in banks:
-                copy(result[:, cols], bank[:])
+        def product(cols, grouped, bank_tag, codes_tag):
+            e_codes = held.tile([P, width(cols)], U32, name=f"e_codes{cols.start}", tag=codes_tag, align_bytes=64)
+            e_scales = held.tile([P, width(cols)], U8, name=f"e_scales{cols.start}", align_bytes=64)
+            bank = psum.tile([P, width(cols)], F32, name=f"out_{bank_tag}", tag=bank_tag)
+            quantize(e_codes[:], e_scales[:], grouped)
+            multiply(bank[:], w2_codes[:], w2_scales[:], e_codes[:], e_scales[:])
+            return cols, bank
 
         def store(lo, hi):
             nc.sync.dma_start(out[:, lo:hi], result[:, lo:hi])
 
-        planes = [pick_planes(cols, tag) for cols, tag in ((B1, "x_codes"), (B2, "planes_free"), (B3, "x_scales"))]
+        early = [pick_planes(C1, BF16, "planes_free"), pick_planes(C2, BF16, "x_codes")]
+        planes = [pick_planes(B2, F32, "w1_scales"), pick_planes(B3, F32, "x_scales")]
         pairs1, pairs2 = pairs_tile(A1), pairs_tile(A2)
         for t in range(PACK):
-            pick_pair(pairs1, t, A1)
-            pick_pair(pairs2, t, A2)
-        first, middle, free = grouped_tile(A1), grouped_tile(slice(A2.start, B1.stop)), grouped_tile(B2)
+            for pairs, cols in ((pairs1, A1), (pairs2, A2)):
+                nc.vector.tensor_copy(pairs[:, t // 2, :, t % 2], looked_up(t, cols))
+        first, middle, free = grouped_tile(A1), grouped_tile(slice(A2.start, C2.stop)), grouped_tile(B2)
+        for tile, cols in zip(early, (C1, C2)):
+            interleave_aside(middle[:, cols.start - A2.start : cols.stop - A2.start, :], tile[:])
+        weave(first[:], pairs1)
+        weave(middle[:, 0 : width(A2), :], pairs2)
+        banks = [product(A1, first[:], "bank_piece0", "codes0")]
+        interleave(free[:], planes[0][:])
+        banks.append(product(slice(256, 512), middle[:, 0:256, :], "bank_piece1", "codes1"))
+        banks.append(product(slice(512, 768), middle[:, 256:512, :], "bank_piece2", "codes2"))
+        banks.append(product(B2, free[:], "bank_piece3", "x_codes"))
         ends = [slice(B3.start, B3.start + 64), slice(B3.start + 64, G)]
-        last = [grouped_tile(cols) for cols in ends]
-        weave(first[:], pairs1, 0, width(A1))
-        weave(middle[:, 0 : width(A2), :], pairs2, 0, width(A2))
-        banks = product([(A1, first[:])], ("bank_piece0",))
-        interleave(middle[:, width(A2) : 512, :], planes[0][:])
-        interleave(free[:], planes[1][:])
-        pieces = [(slice(256, 512), middle[:, 0:256, :]), (slice(512, 768), middle[:, 256:512, :]), (B2, free[:])]
-        banks.extend(product(pieces, ("bank_piece1", "bank_piece2", "bank_piece3")))
+        last = [middle[:, 256 + 64 * k : 256 + 64 * (k + 1), :] for k in range(2)]
         for k in range(2):
-            interleave(last[k][:], planes[2][:, :, 64 * k : 64 * (k + 1)])
-        late = product([(cols, tile[:]) for cols, tile in zip(ends, last)], ("bank1", "bank2"))
+            interleave(last[k], planes[1][:, :, 64 * k : 64 * (k + 1)])
+        late = [product(cols, last[k], f"bank{k + 1}", f"codes_end{k}") for k, cols in enumerate(ends)]
         for cols, bank in banks:
             nc.scalar.copy(result[:, cols], bank[:])
             store(cols.start, cols.stop)
-        empty(nc.scalar.copy, late[:1])
-        empty(nc.vector.tensor_copy, late[1:])
+        nc.scalar.copy(result[:, ends[0]], late[0][1][:])
+        nc.vector.tensor_copy(result[:, ends[1]], late[1][1][:])
         store(B3.start, G)

import concourse.mybir as mybir

D, T, N, H, M, G = 512, 2048, 512, 512, 128, 1024
FLOPS = 2 * D * H * N + 2 * H * M * G

F32 = mybir.dt.float32
BF16 = mybir.dt.bfloat16
I32 = mybir.dt.int32
U32 = mybir.dt.uint32
U16 = mybir.dt.uint16
U8 = mybir.dt.uint8
FP8X4 = mybir.dt.float8_e4m3fn_x4
RELU = mybir.ActivationFunctionType.Relu
COPY = mybir.ActivationFunctionType.Copy
MULT = mybir.AluOpType.mult
ADD = mybir.AluOpType.add

P = 128
PACK = 4
STRIPE = 16
LINE = 4
HALF_N = N // 2
A1, A2 = slice(0, 256), slice(256, 544)
C1, C2 = slice(544, 672), slice(672, 768)
B2, B3 = slice(768, 896), slice(896, 1024)


def width(cols):
    return cols.stop - cols.start


def words(grouped, dtype):
    flat = grouped.rearrange("p c t -> p (c t)").bitcast(dtype)
    return flat.rearrange("p (c u) -> p c u", u=grouped.shape[2] // 2)


def by_column(pairs, dtype):
    return pairs.rearrange("p u c v -> p (u c v)").bitcast(dtype).rearrange("p (u c) -> p c u", u=2)


def tile_attend_hop_pick_kernel(tc, xT, w1, w2, offs, offs2, out):
    nc = tc.nc
    with (
        tc.tile_pool(name="held", bufs=1) as held,
        tc.psum_pool(name="psum", bufs=1) as psum,
    ):
        idx = held.tile([P, N // STRIPE], U16)
        idx2 = held.tile([P, G // STRIPE], U16)
        x_plane = [held.tile([P, T], F32, name=f"x_plane{t}", align_bytes=64) for t in range(PACK)]
        x_codes = held.tile([P, N], U32, tag="x_codes", align_bytes=64)
        x_scales = held.tile([P, N], U8, tag="x_scales", align_bytes=64)
        w1_raw = held.tile([P, PACK, H], F32, align_bytes=64)
        w1_grouped = [held.tile([P, 2, P, PACK], BF16, name=f"w1_grouped{q}", align_bytes=64) for q in range(2)]
        w1_scales = held.tile([P, PACK, P], U8, tag="w1_scales", align_bytes=64)
        w2_raw = held.tile([P, PACK, M], F32, align_bytes=64)
        w2_codes = held.tile([P, M], U32, align_bytes=64)
        w2_scales = held.tile([P, M], U8, align_bytes=64)
        h_plane = [held.tile([P, N], F32, name=f"h_plane{t}", align_bytes=64) for t in range(PACK)]
        result = held.tile([P, G], F32, align_bytes=64)

        x_rows = xT.rearrange("(p t) n -> p t n", t=PACK)
        w1_rows = w1.rearrange("(p j) c -> p j c", j=PACK)
        nc.sync.dma_start(x_plane[0][:], x_rows[:, 0, :])
        nc.sync.dma_start(idx[:], offs)
        for t in range(1, PACK):
            nc.sync.dma_start(x_plane[t][:], x_rows[:, t, :])
        for k in range(2):
            nc.sync.dma_start(w1_raw[:, 2 * k : 2 * k + 2, :], w1_rows[:, 2 * k : 2 * k + 2, :])
        nc.sync.dma_start(idx2[:], offs2)
        nc.sync.dma_start(w2_raw[:], w2.rearrange("(p j) m -> p j m", j=PACK))

        def quantize(codes, scales, grouped):
            nc.vector.quantize_mx(
                out=codes.bitcast(FP8X4),
                scales=scales,
                in_=grouped.rearrange("p c j -> p (c j)"),
            )

        def multiply(bank, left_codes, left_scales, right_codes, right_scales):
            nc.tensor.matmul_mx(
                out=bank,
                lhsT=left_codes.bitcast(FP8X4),
                lhsT_scale=left_scales,
                rhs=right_codes.bitcast(FP8X4),
                rhs_scale=right_scales,
                start=True,
                stop=True,
            )

        def group_w1(copy, rows, q):
            copy(
                w1_grouped[q][:, :, :, rows].rearrange("p v m j -> p m j v"),
                w1_raw[:, rows, :].rearrange("p j (m t) -> p m j t", t=PACK)[:, :, :, 2 * q : 2 * q + 2],
            )

        def quantize_w1(t0, t1):
            q = t0 // 2
            codes = held.tile([P, t1 - t0, P], U32, name=f"w1_codes{t0}", align_bytes=64)
            quantize(
                codes[:].rearrange("p t m -> p (t m)"),
                w1_scales[:, t0:t1, :].rearrange("p t m -> p (t m)"),
                w1_grouped[q][:, t0 - 2 * q : t1 - 2 * q, :, :].rearrange("p t m j -> p (t m) j"),
            )
            return [codes[:, t, :] for t in range(t1 - t0)]

        def first_product(bank, t, codes, cols):
            multiply(bank, codes, w1_scales[:, t, :], x_codes[:, cols], x_scales[:, cols])

        def listed(t, cols):
            return x_plane[t][:].indirect(idx[:, cols.start // STRIPE : cols.stop // STRIPE])

        quarters = [slice(a * P, (a + 1) * P) for a in range(2)]
        upper = slice(HALF_N, N)
        x_picked = [held.tile([P, PACK, P], BF16, name=f"x_picked{a}", align_bytes=64) for a in range(2)]
        x_placed = [held.tile([P, P, PACK], BF16, name=f"x_placed{a}", align_bytes=64) for a in range(2)]
        x_pairs = held.tile([P, 2, HALF_N, 2], BF16, align_bytes=64)
        x_woven = held.tile([P, HALF_N, PACK], BF16, align_bytes=64)
        for t in range(PACK):
            nc.vector.tensor_copy(x_pairs[:, t // 2, :, t % 2], listed(t, upper))
            for picked, placed, cols in zip(x_picked, x_placed, quarters):
                nc.scalar.activation(picked[:, t, :], listed(t, cols), COPY)
                nc.vector.tensor_copy(placed[:, :, t], picked[:, t, :])
        nc.scalar.copy(words(x_woven[:], U32)[:, quarters[0], :], by_column(x_pairs[:], U32)[:, quarters[0], :])
        nc.vector.tensor_copy(words(x_woven[:], I32)[:, quarters[1], :], by_column(x_pairs[:], I32)[:, quarters[1], :])
        for placed, cols in zip(x_placed, quarters):
            quantize(x_codes[:, cols], x_scales[:, cols], placed[:])
        quantize(x_codes[:, upper], x_scales[:, upper], x_woven[:])

        group_w1(nc.scalar.copy, slice(0, 2), 0)
        for t in range(2):
            nc.vector.tensor_copy(
                w1_grouped[0][:, t, :, 2:PACK],
                w1_raw[:, 2:PACK, :].rearrange("p j (m t) -> p t m j", t=PACK)[:, t, :, :],
            )
        group_w1(nc.scalar.copy, slice(0, PACK), 1)

        codes = quantize_w1(0, 1)
        for a in range(PACK):
            cols = slice(a * P, (a + 1) * P)
            bank = psum.tile([P, P], F32, name=f"bank_piece{a}", tag=f"bank_piece{a}")
            first_product(bank[:], 0, codes[0], cols)
            nc.scalar.activation(h_plane[0][:, cols], bank[:], RELU)
        codes.extend(quantize_w1(1, 2))
        w2_grouped = held.tile([P, M, PACK], BF16, align_bytes=64)
        nc.vector.tensor_copy(
            w2_grouped[:].rearrange("p (c i) j -> p c j i", i=LINE),
            w2_raw[:].rearrange("p j (c i) -> p c j i", i=LINE),
        )
        codes.extend(quantize_w1(2, PACK))
        quantize(w2_codes[:], w2_scales[:], w2_grouped[:])
        for t in range(1, PACK):
            bank = psum.tile([P, N], F32, name=f"bank{t}", tag=f"bank{t}")
            first_product(bank[:], t, codes[t], slice(0, N))
            nc.scalar.activation(h_plane[t][:], bank[:], RELU)

        def looked_up(t, cols):
            return h_plane[t][:].indirect(idx2[:, cols.start // STRIPE : cols.stop // STRIPE])

        def grouped_tile(cols):
            return held.tile([P, width(cols), PACK], BF16, name=f"e_grouped{cols.start}", align_bytes=64)

        def pairs_tile(cols):
            return held.tile([P, 2, width(cols), 2], BF16, name=f"e_pairs{cols.start}", align_bytes=64)

        def weave(grouped, pairs):
            nc.vector.tensor_copy(words(grouped, I32), by_column(pairs[:], I32))

        def pick_planes(cols, dtype, tag):
            planes = held.tile([P, PACK, width(cols)], dtype, name=f"e_planes{cols.start}", tag=tag, align_bytes=64)
            for t in range(PACK):
                nc.scalar.activation(planes[:, t, :], looked_up(t, cols), COPY)
            return planes

        def interleave(grouped, planes):
            nc.vector.tensor_copy(
                grouped.rearrange("p (c i) t -> p c t i", i=LINE),
                planes.rearrange("p t (c i) -> p c t i", i=LINE),
            )

        def interleave_aside(grouped, planes):
            nc.gpsimd.tensor_scalar(grouped, planes.rearrange("p t c -> p c t"), 1.0, 0.0, MULT, ADD)

        def product(cols, grouped, bank_tag, codes_tag):
            e_codes = held.tile([P, width(cols)], U32, name=f"e_codes{cols.start}", tag=codes_tag, align_bytes=64)
            e_scales = held.tile([P, width(cols)], U8, name=f"e_scales{cols.start}", align_bytes=64)
            bank = psum.tile([P, width(cols)], F32, name=f"out_{bank_tag}", tag=bank_tag)
            quantize(e_codes[:], e_scales[:], grouped)
            multiply(bank[:], w2_codes[:], w2_scales[:], e_codes[:], e_scales[:])
            return cols, bank

        def store(lo, hi):
            nc.sync.dma_start(out[:, lo:hi], result[:, lo:hi])

        early = [pick_planes(C1, BF16, "planes_free"), pick_planes(C2, BF16, "x_codes")]
        planes = [pick_planes(B2, F32, "w1_scales"), pick_planes(B3, F32, "x_scales")]
        pairs1, pairs2 = pairs_tile(A1), pairs_tile(A2)
        for t in range(PACK):
            for pairs, cols in ((pairs1, A1), (pairs2, A2)):
                nc.vector.tensor_copy(pairs[:, t // 2, :, t % 2], looked_up(t, cols))
        first, middle, free = grouped_tile(A1), grouped_tile(slice(A2.start, C2.stop)), grouped_tile(B2)
        for tile, cols in zip(early, (C1, C2)):
            interleave_aside(middle[:, cols.start - A2.start : cols.stop - A2.start, :], tile[:])
        weave(first[:], pairs1)
        weave(middle[:, 0 : width(A2), :], pairs2)
        banks = [product(A1, first[:], "bank_piece0", "codes0")]
        interleave(free[:], planes[0][:])
        banks.append(product(slice(256, 512), middle[:, 0:256, :], "bank_piece1", "codes1"))
        banks.append(product(slice(512, 768), middle[:, 256:512, :], "bank_piece2", "codes2"))
        banks.append(product(B2, free[:], "bank_piece3", "x_codes"))
        ends = [slice(B3.start, B3.start + 64), slice(B3.start + 64, G)]
        last = [middle[:, 256 + 64 * k : 256 + 64 * (k + 1), :] for k in range(2)]
        for k in range(2):
            interleave(last[k], planes[1][:, :, 64 * k : 64 * (k + 1)])
        late = [product(cols, last[k], f"bank{k + 1}", f"codes_end{k}") for k, cols in enumerate(ends)]
        for cols, bank in banks:
            nc.scalar.copy(result[:, cols], bank[:])
            store(cols.start, cols.stop)
        nc.scalar.copy(result[:, ends[0]], late[0][1][:])
        nc.vector.tensor_copy(result[:, ends[1]], late[1][1][:])
        store(B3.start, G)
